import numpy as np, ml_dtypes
CORES = [8,9,10,11,12,13]
N = 6
import mx_ref
BF = ml_dtypes.bfloat16
def entries(a):
    return np.ascontiguousarray(a.T).reshape(-1)
def table(e):
    return np.ascontiguousarray(np.reshape(e, (-1, 16)).T).astype(np.int32)
def gentries(a):
    return np.ascontiguousarray(a.reshape(8, 16, -1).transpose(0, 2, 1)).reshape(8, -1)
def gtable(e):
    e = np.asarray(e); return np.ascontiguousarray(e.reshape(8, -1, 16).transpose(0, 2, 1)).reshape(128, -1).astype(np.int32)
def tile(rs):
    return np.stack(rs, axis=2).reshape(128, -1).astype(BF)
def cut(t, i, w=512):
    return t[:, w * i:w * i + w]
def f(rng, *shape):
    return mx_ref.flush((rng.standard_normal(shape, dtype=np.float32) * np.exp2(rng.integers(-2, 3, shape[:-1] + (1,)))).astype(BF))
def wide(rng, *shape, cols=0):
    v = rng.standard_normal(shape, dtype=np.float32) * np.exp2(rng.integers(-12, 13, shape)).astype(np.float32)
    if cols: v *= np.repeat(np.exp2(rng.integers(-cols, cols + 1, shape[:-2] + (1, shape[-1] // 4))) * (rng.random(shape[:-2] + (1, shape[-1] // 4)) > 0.0625), 4, axis=-1).astype(np.float32)
    return mx_ref.flush(v.astype(BF))
T, CAPP, P = 512, 64, 256
SL = N * CAPP
G = 8
def pieces(rng, how):
    if how == "ones": n = np.ones((G, SL), int)
    elif how == "full":
        n = T - rng.integers(0, 8, (G, SL)); n[:, ::4] = T
    elif how == "powers":
        k = [1 << i for i in range(T.bit_length())]; k = sorted(set(k + [i + 1 for i in k if i < T]))
        n = rng.permuted(np.tile(np.resize(k, SL), (G, 1)), axis=1)
    else: n = np.where(rng.random((G, SL)) < 0.5, rng.integers(1, T + 1, (G, SL)), np.clip(np.exp2(rng.uniform(0, T.bit_length() - 1, (G, SL))).astype(int), 1, T))
    s = rng.integers(0, T - n + 1)
    if how == "full": s[:] = 0
    if how == "nested":
        for g in range(G):
            for r in range(N):
                m = rng.integers(0, T)
                b = np.sort(rng.choice(rng.integers(0, m + 1, 16), CAPP)); e = np.sort(rng.choice(rng.integers(m, T, 16), CAPP))[::-1]
                k = r * CAPP + rng.permutation(CAPP); s[g, k] = b; n[g, k] = e - b + 1
    return s, n
def lists(rng, how="any", every=False):
    held = np.zeros((N, N, CAPP), bool)
    for r in range(N):
        n = rng.integers(0, CAPP + 1, N); n[(r + rng.integers(1, N)) % N] = CAPP
        for q in range(N): held[q, r, rng.permutation(CAPP)[:CAPP if every else n[q]]] = True
    d = {"lo": [], "ln": [], "pf": [], "pg": []}
    for q in range(N):
        s, n = pieces(rng, how); e = ~held[q].reshape(-1)
        s[:, e] = -1; n[:, e] = 0
        d["lo"].append(gtable(s)); d["ln"].append(gtable(n))
    who = rng.permutation(N)
    for r in range(N):
        k = rng.permutation(np.flatnonzero(held[:, r]))
        first = rng.permutation(np.resize(k, P))
        second = np.where(rng.random(P) < 0.25, -1, rng.choice(k, P))
        if how == "ones":
            if r == who[0]:
                first[rng.permutation(P)[:P // 2]] = k[0]; second[rng.permutation(P)[:P // 2]] = k[0]
            if r == who[1]: second[:] = -1
            if r == who[2]: second = rng.choice(k, P)
        d["pf"].append(table(first))
        d["pg"].append(table(second))
    return {k: np.stack(t) for k, t in d.items()}
def setup_inputs(rng):
    return {"x": f(rng, N, 128, 4 * T), "a": f(rng, N, 128, 2048), "u": f(rng, N, 128, 512), "v": f(rng, N, 128, 512), **lists(rng)}
def setup_inputs_ones(rng):
    return {**setup_inputs(rng), **lists(rng, "ones")}
def setup_inputs_full(rng):
    return {**setup_inputs(rng), **lists(rng, "full", True)}
def setup_inputs_powers(rng):
    return {**setup_inputs(rng), **lists(rng, "powers", True)}
def setup_inputs_nested(rng):
    return {**setup_inputs(rng), **lists(rng, "nested", True)}
def setup_inputs_spread(rng):
    d = setup_inputs(rng); d["x"] = wide(rng, N, 128, 4 * T, cols=8); return d
def check_inputs(d):
    b = []; held = []
    for q in range(N):
        s, n = gentries(d["lo"][q]).reshape(G, -1), gentries(d["ln"][q]).reshape(G, -1)
        e = s == -1; held.append(~e[0])
        if s.min() < -1 or s.max() >= T or (e != e[:1]).any(): b.append("lo")
        if (n[e] != 0).any() or (n[~e] < 1).any() or (n[~e] > T - s[~e]).any(): b.append("ln")
    for r in range(N):
        h = np.concatenate([held[q][r * CAPP:r * CAPP + CAPP] for q in range(N)])
        for k, least in (("pf", 0), ("pg", -1)):
            j = entries(d[k][r])
            if j.min() < least or j.max() >= SL or not h[j[(j >= 0) & (j < SL)]].all(): b.append(k)
    return b
def reference(x, a, u, v, lo, ln, pf, pg):
    sent = []
    for q in range(N):
        X = mx_ref.quantize(x[q])
        Z = np.stack([mx_ref.matmul(mx_ref.quantize(np.ascontiguousarray(cut(a[q], i))), X) for i in range(4)])
        h = np.maximum(Z, np.float32(0)) * np.float32(0.05)
        s, n = gentries(lo[q]), gentries(ln[q])
        R = np.zeros((4, 128, SL), np.float32)
        for k in range(SL):
            for g in range(8):
                if n[g, k]: R[:, 16 * g:16 * g + 16, k] = h[:, 16 * g:16 * g + 16, s[g, k]:s[g, k] + n[g, k]].max(axis=2)
        sent.append([mx_ref.quantize(np.ascontiguousarray(tile([R[i][:, CAPP * r:CAPP * r + CAPP] for i in range(4)]))) for r in range(N)])
    y = np.zeros((N, 128, P), np.float32)
    for r in range(N):
        V, U = mx_ref.quantize(v[r]), mx_ref.quantize(u[r])
        zv = np.concatenate([mx_ref.matmul(V, sent[q][r]) for q in range(N)], axis=1)
        zu = np.concatenate([mx_ref.matmul(U, sent[q][r]) for q in range(N)], axis=1)
        first, second = entries(pf[r]), entries(pg[r])
        y[r] = zv[:, first]
        two = second >= 0
        y[r][:, two] += zu[:, second[two]]
    return {"y": y}

@@ -1,0 +1,402 @@
+from concourse.bass import DstId, RemoteDMATransfer
+from concourse.mybir import dt, AluOpType, ActivationFunctionType
+
+N, T_COLS, CAPP, P = 6, 512, 64, 256
+SL = N * CAPP
+NS = SL // 16
+CC = CAPP // 16
+B = 6
+ST = 528
+NB = ST // B
+LV = 6
+XC = 43 * B
+S6, P6 = 2 * ST, 4 * ST
+W = 4768
+CE, DE = -ST, -3 * ST
+EP, ES = W + DE, W + CE
+RG = ES + 2 * ST
+
+FAR, NEAR = 3 * CAPP, 2 * CAPP
+CH = {"a": (0, FAR + NEAR), "f": (0, FAR), "n": (FAR, NEAR), "o": (FAR + NEAR, CAPP)}
+WORK = {(0, "a"): 3, (1, "f"): 3, (2, "f"): 3, (3, "f"): 3, (1, "n"): 3, (2, "n"): 3, (3, "n"): 3,
+        (0, "o"): 3, (1, "o"): 3, (2, "o"): 3, (3, "o"): 3}
+
+SCRATCH = {
+    "xb": ("sbuf", [128, 2048], "bfloat16"), "ab": ("sbuf", [128, 2048], "bfloat16"),
+    "ub": ("sbuf", [128, 512], "bfloat16"), "vb": ("sbuf", [128, 512], "bfloat16"),
+    "xq": ("sbuf", [128, 512], "float8_e4m3fn_x4"), "xs": ("sbuf", [128, 512], "uint8"),
+    "aq": ("sbuf", [128, 512], "float8_e4m3fn_x4"), "sa": ("sbuf", [128, 512], "uint8"),
+    "uq": ("sbuf", [128, 128], "float8_e4m3fn_x4"), "us": ("sbuf", [128, 128], "uint8"),
+    "vq": ("sbuf", [128, 128], "float8_e4m3fn_x4"), "vs": ("sbuf", [128, 128], "uint8"),
+    "cq": ("sbuf", [128, 320], "float8_e4m3fn_x4"), "cs": ("sbuf", [128, 320], "uint8"),
+    "oq": ("sbuf", [128, 128], "float8_e4m3fn_x4"), "ow": ("sbuf", [128, 128], "uint8"),
+    "rq": ("sbuf", [128, 320], "float8_e4m3fn_x4"), "rs": ("sbuf", [128, 320], "uint8"),
+    "win": ("sbuf", [128, 2 * RG], "bfloat16"),
+    "tile": ("sbuf", [128, 4 * SL], "bfloat16"),
+    "ones": ("sbuf", [128, 960], "bfloat16"), "m6": ("sbuf", [128, ST], "bfloat16"),
+    "m3": ("sbuf", [128, 960], "bfloat16"), "m2": ("sbuf", [128, 640], "bfloat16"),
+    "mc": ("sbuf", [128, 6 * 2 * NB], "bfloat16"), "aw": ("sbuf", [128, LV * NS], "bfloat16"),
+    "ll": ("sbuf", [128, 2 * NS], "int32"), "lm": ("sbuf", [128, NS], "float32"),
+    "ld": ("sbuf", [128, 4 * NS], "float32"), "l6": ("sbuf", [128, 2 * NS], "int32"), "sb": ("sbuf", [128, 2 * NS], "int32"),
+    "sh": ("sbuf", [128, 2 * LV * NS], "int32"), "fl": ("sbuf", [128, LV * NS], "bfloat16"),
+    "cn": ("sbuf", [128, LV * NS], "float32"), "ee": ("sbuf", [128, 2 * NS], "float32"),
+    "yy": ("sbuf", [128, 2 * NS], "float32"), "xm": ("sbuf", [128, 2 * NS], "float32"),
+    "dd": ("sbuf", [128, 2 * NS], "float32"), "fd": ("sbuf", [128, 2 * NS], "float32"),
+    "of": ("sbuf", [128, 4 * NS], "float32"), "oa": ("sbuf", [128, 2 * NS], "uint16"), "oc": ("sbuf", [128, 2 * NS], "uint16"),
+    "pl": ("sbuf", [128, 32], "int32"), "pz": ("sbuf", [128, 16], "int32"), "pu": ("sbuf", [128, 32], "uint16"),
+    "zu": ("sbuf", [128, 400], "float32"), "zv": ("sbuf", [128, 384], "float32"),
+    "gu": ("sbuf", [128, P], "float32"), "yb": ("sbuf", [128, P], "float32"),
+    "zp": ("psum", [128, 2048], "float32"), "pp": ("psum", [128, 2048], "float32"),
+}
+for (_i, _h), _w in WORK.items():
+    SCRATCH["g%d%s" % (_i, _h)] = ("sbuf", [128, _w * CH[_h][1]], "bfloat16")
+    SCRATCH["s%d%s" % (_i, _h)] = ("sbuf", [128, _w * CH[_h][1]], "bfloat16")
+SEMAPHORES = ["cv", "cs_", "ct", "cg", "lists", "x0", "x1", "a0", "a1", "a2", "uv", "pfg", "y0", "y1", "arr0", "arr1", "sent"]
+
+
+def order(q):
+    return [(q + 1 + k) % N for k in range(N)]
+
+
+def places(r):
+    return [(r + 3 + k) % N for k in range(3)] + [(r + 1 + k) % N for k in range(2)]
+
+
+def runs(ranks):
+    out = []
+    for k, q in enumerate(ranks):
+        if out and out[-1][1] + out[-1][2] == q:
+            out[-1][2] += 1
+        else:
+            out.append([k, q, 1])
+    return out
+
+
+def sending(q, T, topo):
+    out = []
+    for ds in (order(q)[0:3], order(q)[3:5]):
+        eng = topo.engines(T.cores[q], T.cores[ds[0]])
+        ev, od = eng[0::2], eng[1::2]
+        k = len(ev) // 2
+        ds = sorted(ds, key=lambda r: topo.die(T.cores[r]) == topo.die(T.cores[q]))
+        es = ([ev[:k], ev[k:], od], [od[:k], od[k:], ev]) if len(ds) == 3 else ([ev, od], [od, ev])
+        out.append([[(r, e) for r, e in zip(ds, x)] for x in es])
+    return out
+
+
+def rank_program(g, core, T, topo):
+    rank = T.rank_of(core)
+    if rank is None:
+        return
+    A, F = AluOpType, ActivationFunctionType
+    que = {"cv": g.vector, "cs_": g.scalar, "ct": g.tensor, "cg": g, "sy": g.sync}
+    count = {k: 0 for k in que}
+    seen = {k: {} for k in que}
+    v, s, t = g.vector, g.scalar, g.tensor
+
+    def need(q, *toks):
+        for sem, val in toks:
+            if seen[q].get(sem, 0) < val:
+                que[q].wait_ge(T.sem[sem], val)
+                seen[q][sem] = val
+
+    def done(q, ins):
+        ins.then_inc(T.sem[q], 1)
+        count[q] += 1
+        return (q, count[q])
+
+    s.dma_start(T.ll[:, NS:2 * NS], T.ln[:]).then_inc(T.sem.lists, 16)
+    g.sync.dma_start(T.ll[:, 0:NS], T.lo[:]).then_inc(T.sem.lists, 16)
+    g.sync.dma_start(T.xb[:, 0:4 * XC], T.x[:, 0:4 * XC]).then_inc(T.sem.x0, 16)
+    s.dma_start(T.ab[:, 0:512], T.a[:, 0:512]).then_inc(T.sem.a0, 16)
+    g.sync.dma_start(T.xb[:, 4 * XC:2048], T.x[:, 4 * XC:2048]).then_inc(T.sem.x1, 16)
+    g.sync.dma_start(T.ab[:, 512:1024], T.a[:, 512:1024]).then_inc(T.sem.a1, 16)
+    g.sync.dma_start(T.ab[:, 1024:2048], T.a[:, 1024:2048]).then_inc(T.sem.a2, 16)
+    g.sync.dma_start(T.ub[:], T.u[:]).then_inc(T.sem.uv, 16)
+    g.sync.dma_start(T.vb[:], T.v[:]).then_inc(T.sem.uv, 16)
+    for k in range(8):
+        g.sync.dma_start(T.pl[16 * k:16 * k + 16, 0:16], T.pf[:]).then_inc(T.sem.pfg, 16)
+        g.sync.dma_start(T.pl[16 * k:16 * k + 16, 16:32], T.pg[:]).then_inc(T.sem.pfg, 16)
+
+    k_one = done("cv", v.memset(T.ones[:], 1.0))
+    k_mo = done("cv", v.memset(T.mc[:, 3 * 2 * NB:6 * 2 * NB], 1.0))
+    k_aw = done("cv", v.memset(T.aw[:], 1.0))
+    k_zu = done("cv", v.memset(T.zu[:, 384:400], 0.0))
+    need("cv", k_aw)
+    done("cv", v.memset(T.aw[:, 0::LV], 0.0))
+    k_aw = done("cv", v.memset(T.aw[:, 1::LV], float(W)))
+
+    need("cg", k_one)
+
+    def mask(out, n, b):
+        return done("cg", g.affine_select(out, T.ones[:, 0:n], [[0, n // b], [1, b]], A.is_gt, 0.0, 0, 0))
+
+    k_m6 = mask(T.m6[:], ST, B)
+    for m in range(1, 4):
+        k_mc = mask(T.mc[:, 2 * NB * (m - 1):2 * NB * m], 2 * NB, 1 << m)
+    k_ms = {3: mask(T.m3[:], 960, 3)}
+    if 2 in WORK.values():
+        k_ms[2] = mask(T.m2[:], 640, 2)
+
+    def zero(out, n):
+        return done("cs_", s.activation(out, T.ones[:, 0:n], F.Copy, scale=0.0))
+
+    need("cs_", k_one)
+    for i in range(4):
+        b = (i // 2) * RG + (i % 2) * ST
+        k_hp = zero(T.win[:, b + T_COLS:b + ST], ST - T_COLS)
+    for p in range(2):
+        zero(T.win[:, p * RG + 6 * ST:p * RG + EP + LV], EP + LV - 6 * ST)
+        zero(T.win[:, p * RG + ES + 2 * ST - LV:p * RG + RG], LV)
+    need("cs_", k_mo)
+    for m in range(4, 7):
+        for p in range(2):
+            b = 2 * NB * (m - 1) + NB * p
+            k_mz = zero(T.mc[:, b:b + NB:1 << m], len(range(0, NB, 1 << m)))
+
+    c = CC * ((rank + 1) % N)
+    cuts = [(0, c, NS - c)] + ([(NS - c, 0, c)] if c else [])
+    need("cv", ("lists", 32))
+    for o, b, n in cuts:
+        done("cv", v.tensor_copy(T.ld[:, NS + o:NS + o + n], T.ll[:, b:b + n]))
+    for o, b, n in cuts:
+        k_lm = done("cv", v.tensor_scalar(T.lm[:, o:o + n], T.ll[:, NS + b:NS + b + n], -1, None, A.add))
+    LR = T.ld[:, NS:3 * NS]
+    need("cv", k_lm)
+    k = done("cv", v.tensor_tensor(T.ld[:, 2 * NS:3 * NS], T.ld[:, NS:2 * NS], T.lm[:], A.add))
+    need("cv", k)
+    k = done("cv", v.tensor_scalar(T.l6[:], LR, 171, None, A.mult))
+    need("cs_", k_lm)
+    done("cs_", s.activation(T.ee[:, 0:NS], T.lm[:], F.Sign))
+    k_ee = done("cs_", s.activation(T.ee[:, NS:2 * NS], T.lm[:], F.Sign, scale=-1.0))
+    need("cv", k)
+    k = done("cv", v.tensor_scalar(T.sb[:], T.l6[:], 10, None, A.arith_shift_right))
+    for j in range(3):
+        done("cv", v.tensor_scalar(T.sh[:, j::LV], T.l6[:], 11 + j, None, A.arith_shift_right))
+    need("cv", k)
+    done("cv", v.tensor_scalar(T.ld[:, 0:NS], T.sb[:, 0:NS], B, CE, A.mult, A.add))
+    k_ld = done("cv", v.tensor_scalar(T.ld[:, 3 * NS:4 * NS], T.sb[:, NS:2 * NS], B, DE, A.mult, A.add))
+
+    def quant(out, sc, src, *deps):
+        need("cv", *deps)
+        return done("cv", v.quantize_mx(out, sc, src))
+
+    k_x0 = quant(T.xq[:, 0:XC], T.xs[:, 0:XC], T.xb[:, 0:4 * XC], ("x0", 16))
+    need("cv", k_ld)
+    k = done("cv", v.tensor_tensor(T.dd[:], T.ld[:, 0:2 * NS], T.ld[:, 2 * NS:4 * NS], A.subtract))
+    k_a = [quant(T.aq[:, 0:128], T.sa[:, 0:128], T.ab[:, 0:512], ("a0", 16))]
+    need("cv", k)
+    done("cv", v.tensor_scalar(T.fd[:, 0:NS], T.dd[:, 0:NS], CE - (B - 1), S6, A.is_le, A.mult))
+    k = done("cv", v.tensor_scalar(T.fd[:, NS:2 * NS], T.dd[:, NS:2 * NS], -DE, P6, A.is_le, A.mult))
+    for j in range(3, LV):
+        k_sh = done("cv", v.tensor_scalar(T.sh[:, j::LV], T.l6[:], 11 + j, None, A.arith_shift_right))
+    need("cv", k)
+    k = done("cv", v.tensor_tensor(T.of[:, 0:2 * NS], LR, T.fd[:], A.add))
+    k_x1 = quant(T.xq[:, XC:512], T.xs[:, XC:512], T.xb[:, 4 * XC:2048], ("x1", 16))
+    need("cv", k)
+    k_oa = done("cv", v.tensor_copy(T.oa[:], T.of[:, 0:2 * NS]))
+
+    def levels():
+        need("cv", k_sh)
+        return done("cv", v.tensor_tensor(T.fl[:], T.sh[:, 0:LV * NS], T.sh[:, LV * NS:2 * LV * NS], A.not_equal))
+
+    def offsets(k):
+        need("cv", k, k_aw)
+        k = done("cv", v.tensor_tensor_scan(T.cn[:], T.aw[:], T.fl[:], 0.0, A.mult, A.add))
+        need("cv", k_ee)
+        done("cv", v.tensor_tensor(T.yy[:], LR, T.ee[:], A.add))
+        need("cv", k)
+        done("cv", v.tensor_tensor(T.xm[:, 0:NS], T.ld[:, 0:NS], T.cn[:, LV - 1::LV], A.add))
+        k = done("cv", v.tensor_tensor(T.xm[:, NS:2 * NS], T.ld[:, 3 * NS:4 * NS], T.cn[:, LV - 1::LV], A.add))
+        need("cv", k)
+        k = done("cv", v.tensor_tensor(T.of[:, 2 * NS:4 * NS], T.xm[:], T.yy[:], A.max))
+        need("cv", k)
+        return done("cv", v.tensor_copy(T.oc[:], T.of[:, 2 * NS:4 * NS]))
+
+    def mm(out, w, ws, x, xs, *deps):
+        need("ct", *deps)
+        return done("ct", t.matmul_mx(out, w, ws, x, xs, True, True))
+
+    def at(i):
+        return (i // 2) * RG + (i % 2) * ST
+
+    def relu(i, c, n, src, *deps):
+        need("cs_", *deps)
+        return done("cs_", s.activation(T.win[:, at(i) + c:at(i) + c + n], src, F.Relu, scale=0.05))
+
+    k0 = mm(T.zp[:, 0:XC], T.aq[:, 0:128], T.sa[:, 0:128], T.xq[:, 0:XC], T.xs[:, 0:XC], k_x0, k_a[0])
+    k1 = mm(T.pp[:, 1536:2048 - XC], T.aq[:, 0:128], T.sa[:, 0:128], T.xq[:, XC:512], T.xs[:, XC:512], k_x1)
+    k_h = {0: relu(0, 0, XC, T.zp[:, 0:XC], k0), 4: relu(0, XC, 512 - XC, T.pp[:, 1536:2048 - XC], k1)}
+
+    def product(i):
+        return mm(T.zp[:, 512 * i:512 * i + 512], T.aq[:, 128 * i:128 * i + 128], T.sa[:, 128 * i:128 * i + 128], T.xq[:], T.xs[:], k_a[i])
+
+    def empty(i, k):
+        k_h[i] = relu(i, 0, 512, T.zp[:, 512 * i:512 * i + 512], k)
+
+    def prefix(i, a, b, *deps):
+        w = at(i)
+        need("cv", k_m6, k_hp, *deps)
+        return done("cv", v.tensor_tensor_scan(T.win[:, w + P6 + a:w + P6 + b], T.m6[:, a:b], T.win[:, w + a:w + b], 0.0, A.mult, A.max))
+
+    def suffix(i, *deps):
+        w = at(i)
+        need("cv", k_m6, k_hp, *deps)
+        end = w - 1 if w else None
+        return done("cv", v.tensor_tensor_scan(T.win[:, w + S6 + ST - 1:w + S6 - 1:-1], T.m6[:], T.win[:, w + ST - 1:end:-1], 0.0, A.mult, A.max))
+
+    def coarse(p, k_p):
+        b, n = p * RG, 2 * NB
+        need("cv", k_mc, k_mz, k_p)
+        for m in range(1, 7):
+            o = n * (m - 1)
+            done("cv", v.tensor_tensor_scan(T.win[:, b + EP + LV + m - 1:b + EP + 2 * ST:LV], T.win[:, b + P6 + B - 1:b + P6 + 2 * ST - B:B],
+                                            T.mc[:, o + 1:o + n], 0.0, A.max, A.mult))
+            tok = done("cv", v.tensor_tensor_scan(T.win[:, b + ES + LV * (n - 2) + m - 1:b + ES - 1:-LV], T.win[:, b + P6 + 2 * ST - 1:b + P6 + B:-B],
+                                                  T.mc[:, o + n - 1:o:-1], 0.0, A.max, A.mult))
+        return tok
+
+    WIN = [S6 + ST, P6 + ST, ES + ST, EP + ST]
+
+    def part(i, e, c, n):
+        o = (e % 2) * NS + c // 16
+        return T.win[:, at(i):at(i) + WIN[e]].indirect((T.oa if e < 2 else T.oc)[:, o:o + n // 16])
+
+    tok = {}
+
+    def gather(i, h, es, *deps):
+        w, (c, n) = WORK[i, h], CH[h]
+        for e in es:
+            if e < w:
+                need("cs_", *deps)
+                tok[i, h] = done("cs_", s.activation(T["g%d%s" % (i, h)][:, e:w * n:w], part(i, e, c, n), F.Copy))
+
+    def best(i, h):
+        w, (c, n) = WORK[i, h], CH[h]
+        need("cv", k_ms[w], tok[i, h])
+        msk, src, dst = T["m%d" % w], T["g%d%s" % (i, h)], T["s%d%s" % (i, h)]
+        k = done("cv", v.tensor_tensor_scan(dst[:, 0:w * n], msk[:, 0:w * n], src[:, 0:w * n], 0.0, A.mult, A.max))
+        if w == 2:
+            need("cv", k)
+            k = done("cv", v.tensor_tensor(src[:, 0:n], part(i, 2, c, n), dst[:, 1:2 * n:2], A.max))
+        return k
+
+    def last(i, h, k):
+        w, (c, n) = WORK[i, h], CH[h]
+        need("cv", k)
+        cur = T["s%d%s" % (i, h)][:, 2:3 * n:3] if w == 3 else T["g%d%s" % (i, h)][:, 0:n]
+        return done("cv", v.tensor_tensor(T.tile[:, 4 * c + i:4 * (c + n):4], part(i, 3, c, n), cur, A.max))
+
+    def merge(*todo):
+        b = best(*todo[0])
+        for j, x in enumerate(todo):
+            n = best(*todo[j + 1]) if j + 1 < len(todo) else None
+            k = last(*x, b)
+            b = n
+        return k
+
+    def pack(c, n, k):
+        return quant(T.cq[:, c:c + n], T.cs[:, c:c + n], T.tile[:, 4 * c:4 * (c + n)], k)
+
+    prefix(0, 0, XC, k_h[0])
+    k_a.append(quant(T.aq[:, 128:256], T.sa[:, 128:256], T.ab[:, 512:1024], ("a1", 16)))
+    empty(1, product(1))
+    k_f = levels()
+    ks0 = suffix(0, k_h[4])
+    prefix(0, XC, ST)
+    k_oc = offsets(k_f)
+    k_a.append(quant(T.aq[:, 256:512], T.sa[:, 256:512], T.ab[:, 1024:2048], ("a2", 16)))
+    k_a.append(k_a[2])
+    z2, z3 = product(2), product(3)
+    ks1 = suffix(1, k_h[1])
+    kp1 = prefix(1, 0, ST)
+    t01 = coarse(0, kp1)
+    gather(0, "a", (0,), k_oa, ks0, k_h[1])
+    gather(0, "a", (1,), ks1)
+    empty(2, z2)
+    empty(3, z3)
+    gather(1, "f", (0, 1), kp1)
+    gather(0, "a", (2,), k_oc, t01)
+    gather(1, "f", (2,))
+    ks2, kp2 = suffix(2, k_h[2]), prefix(2, 0, ST)
+    ks3, kp3 = suffix(3, k_h[3]), prefix(3, 0, ST)
+    t23 = coarse(1, kp3)
+    gather(2, "f", (0, 1), ks3)
+    gather(3, "f", (0, 1), kp3)
+    for i, h in ((2, "f"), (3, "f")):
+        gather(i, h, (2,), t23)
+    for i, h in ((1, "n"), (2, "n"), (3, "n"), (0, "o"), (1, "o"), (2, "o"), (3, "o")):
+        gather(i, h, (0, 1, 2))
+    merge((0, "a"))
+    k_c0 = pack(0, FAR, merge((1, "f"), (2, "f"), (3, "f")))
+    k_c1 = pack(FAR, NEAR, merge((1, "n"), (2, "n"), (3, "n")))
+
+    sent = 0
+    for h, (k, half) in enumerate(zip((k_c0, k_c1), sending(rank, T, topo))):
+        need("cg", k)
+        for what in (0, 1):
+            trs = []
+            for r, es in half[what]:
+                rid, pnc = topo.addr(T.cores[r])[0:2]
+                msk = 0
+                for e in es:
+                    msk |= 1 << e
+                a, b = CAPP * order(rank).index(r), CAPP * places(r).index(rank)
+                if what == 0:
+                    src, out = T.cq[:, a:a + CAPP].bitcast(dt.uint8), T.rq[:, b:b + CAPP].bitcast(dt.uint8)
+                else:
+                    src, out = T.cs[:, a:a + CAPP], T.rs[:, b:b + CAPP]
+                trs.append(RemoteDMATransfer(dst_ids=[DstId(rid=rid, pnc=pnc)], dma_engine_mask=msk, remote_sem=T.sem["arr%d" % h], src=src, dst=out))
+                sent += len(es)
+            g.remote_dma_fused(trs, local_sem=T.sem.sent)
+    arrive = [0, 0]
+    for q in range(N):
+        if q != rank:
+            for h, half in enumerate(sending(q, T, topo)):
+                for what in half:
+                    arrive[h] += sum(len(es) for r, es in what if r == rank)
+
+    k_u = quant(T.uq[:], T.us[:], T.ub[:], ("uv", 32))
+    k_v = quant(T.vq[:], T.vs[:], T.vb[:], ("uv", 32))
+    need("cv", ("pfg", 256))
+    k = done("cv", v.tensor_scalar(T.pz[:], T.pl[:, 16:32], 0, SL, A.is_lt, A.mult))
+    merge((0, "o"))
+    need("cv", k)
+    k = done("cv", v.tensor_tensor(T.pl[:, 16:32], T.pl[:, 16:32], T.pz[:], A.max))
+    merge((1, "o"))
+    need("cv", k)
+    k_pu = done("cv", v.tensor_copy(T.pu[:], T.pl[:]))
+    k_co = quant(T.oq[:], T.ow[:], T.tile[:, 4 * (SL - 128):4 * SL], merge((2, "o"), (3, "o")))
+
+    ku = mm(T.pp[:, 0:FAR], T.uq[:], T.us[:], T.rq[:, 0:FAR], T.rs[:, 0:FAR], k_u, k_v, ("arr0", arrive[0]))
+    kv = mm(T.pp[:, 512:512 + FAR], T.vq[:], T.vs[:], T.rq[:, 0:FAR], T.rs[:, 0:FAR])
+    kuo = mm(T.pp[:, 1024:1152], T.uq[:], T.us[:], T.oq[:], T.ow[:], k_co)
+    kvo = mm(T.pp[:, 1536:1664], T.vq[:], T.vs[:], T.oq[:], T.ow[:])
+
+    def natural(q, out, src, ranks, c, k):
+        need(q, k)
+        for o, r, n in runs(ranks):
+            d, x = out[:, CAPP * r:CAPP * (r + n)], src[:, c + CAPP * o:c + CAPP * (o + n)]
+            tok = done(q, s.activation(d, x, F.Copy) if q == "cs_" else v.tensor_copy(d, x))
+        return tok
+
+    far, near = places(rank)[0:3], places(rank)[3:5]
+    natural("cs_", T.zu, T.pp, far, 0, ku)
+    natural("cv", T.zv, T.pp, far, 512, kv)
+    natural("cs_", T.zu, T.pp, [rank], 1024 + 128 - CAPP, kuo)
+    natural("cv", T.zv, T.pp, [rank], 1536 + 128 - CAPP, kvo)
+
+    ku = mm(T.zp[:, 0:NEAR], T.uq[:], T.us[:], T.rq[:, FAR:320], T.rs[:, FAR:320], ("arr1", arrive[1]))
+    kv = mm(T.zp[:, 512:512 + NEAR], T.vq[:], T.vs[:], T.rq[:, FAR:320], T.rs[:, FAR:320])
+    k_zu2 = natural("cs_", T.zu, T.zp, near, 0, ku)
+    k_zv = natural("cv", T.zv, T.zp, near, 512, kv)
+    need("cs_", k_pu, k_zu, k_zu2)
+    k_g = [done("cs_", s.activation(T.gu[:, 128 * h:128 * h + 128], T.zu[:].indirect(T.pu[:, 16 + 8 * h:24 + 8 * h]), F.Copy)) for h in (0, 1)]
+    need("cv", k_zv)
+    for h in (0, 1):
+        need("cv", k_g[h])
+        k = done("cv", v.tensor_tensor(T.yb[:, 128 * h:128 * h + 128], T.zv[:].indirect(T.pu[:, 8 * h:8 * h + 8]), T.gu[:, 128 * h:128 * h + 128], A.add))
+        need("sy", k)
+        g.sync.dma_start(T.y[:, 128 * h:128 * h + 128], T.yb[:, 128 * h:128 * h + 128]).then_inc(T.sem["y%d" % h], 16)
+    g.wait_ge(T.sem.sent, sent)
+    need("sy", ("cs_", count["cs_"]), ("ct", count["ct"]), ("cg", count["cg"]), ("y0", 16), ("y1", 16))

@@ -4,22 +4,25 @@ from concourse.mybir import dt, AluOpType, ActivationFunctionType
 N, T_COLS, CAPP, P = 6, 512, 64, 256
 SL = N * CAPP
 NS = SL // 16
-CC = CAPP // 16
 B = 6
 ST = 528
-NB = ST // B
+NB, USED = ST // B, 86
 LV = 6
 XC = 43 * B
-S6, P6 = 2 * ST, 4 * ST
-W = 4768
-CE, DE = -ST, -3 * ST
-EP, ES = W + DE, W + CE
-RG = ES + 2 * ST
+J = 2 * ST
+S0, H0, P0, RG = 0, J, 2 * J, 4 * J
+K = J + 2 * B - 1
+E0 = H0 + 2 * K - B - 1
+BIG = 1e29
+PHI, LESS = float(2 ** 23 + 1), 1.0 - 2.0 ** -24
 
-FAR, NEAR = 3 * CAPP, 2 * CAPP
-CH = {"a": (0, FAR + NEAR), "f": (0, FAR), "n": (FAR, NEAR), "o": (FAR + NEAR, CAPP)}
-WORK = {(0, "a"): 3, (1, "f"): 3, (2, "f"): 3, (3, "f"): 3, (1, "n"): 3, (2, "n"): 3, (3, "n"): 3,
-        (0, "o"): 3, (1, "o"): 3, (2, "o"): 3, (3, "o"): 3}
+
+def shift(m):
+    return (2 ** m + 2) // 3
+
+
+CH = {"a": (0, 128), "b": (128, 128), "m": (256, 64), "o": (320, 64)}
+WORK = {("a", 0): 2, ("a", 1): 2, ("b", 0): 3, ("b", 1): 3, ("m", 0): 3, ("m", 1): 3, ("o", 0): 3, ("o", 1): 3}
 
 SCRATCH = {
     "xb": ("sbuf", [128, 2048], "bfloat16"), "ab": ("sbuf", [128, 2048], "bfloat16"),
@@ -28,60 +31,30 @@ SCRATCH = {
     "aq": ("sbuf", [128, 512], "float8_e4m3fn_x4"), "sa": ("sbuf", [128, 512], "uint8"),
     "uq": ("sbuf", [128, 128], "float8_e4m3fn_x4"), "us": ("sbuf", [128, 128], "uint8"),
     "vq": ("sbuf", [128, 128], "float8_e4m3fn_x4"), "vs": ("sbuf", [128, 128], "uint8"),
-    "cq": ("sbuf", [128, 320], "float8_e4m3fn_x4"), "cs": ("sbuf", [128, 320], "uint8"),
+    "cq": ("sbuf", [128, 384], "float8_e4m3fn_x4"), "cs": ("sbuf", [128, 384], "uint8"),
     "oq": ("sbuf", [128, 128], "float8_e4m3fn_x4"), "ow": ("sbuf", [128, 128], "uint8"),
-    "rq": ("sbuf", [128, 320], "float8_e4m3fn_x4"), "rs": ("sbuf", [128, 320], "uint8"),
+    "rq": ("sbuf", [128, 320], "float8_e4m3fn_x4"), "rs": ("sbuf", [128, 512], "uint8"),
     "win": ("sbuf", [128, 2 * RG], "bfloat16"),
     "tile": ("sbuf", [128, 4 * SL], "bfloat16"),
-    "ones": ("sbuf", [128, 960], "bfloat16"), "m6": ("sbuf", [128, ST], "bfloat16"),
-    "m3": ("sbuf", [128, 960], "bfloat16"), "m2": ("sbuf", [128, 640], "bfloat16"),
-    "mc": ("sbuf", [128, 6 * 2 * NB], "bfloat16"), "aw": ("sbuf", [128, LV * NS], "bfloat16"),
-    "ll": ("sbuf", [128, 2 * NS], "int32"), "lm": ("sbuf", [128, NS], "float32"),
-    "ld": ("sbuf", [128, 4 * NS], "float32"), "l6": ("sbuf", [128, 2 * NS], "int32"), "sb": ("sbuf", [128, 2 * NS], "int32"),
-    "sh": ("sbuf", [128, 2 * LV * NS], "int32"), "fl": ("sbuf", [128, LV * NS], "bfloat16"),
-    "cn": ("sbuf", [128, LV * NS], "float32"), "ee": ("sbuf", [128, 2 * NS], "float32"),
-    "yy": ("sbuf", [128, 2 * NS], "float32"), "xm": ("sbuf", [128, 2 * NS], "float32"),
+    "ones": ("sbuf", [128, ST], "bfloat16"), "m6": ("sbuf", [128, ST], "bfloat16"),
+    "m3": ("sbuf", [128, 384], "bfloat16"), "m2": ("sbuf", [128, 512], "bfloat16"),
+    "ll": ("sbuf", [128, 4 * NS], "int32"), "qq": ("sbuf", [128, 6 * NS], "float32"),
+    "l6": ("sbuf", [128, 2 * NS], "int32"), "sb": ("sbuf", [128, 2 * NS], "int32"), "b6": ("sbuf", [128, 2 * NS], "float32"),
+    "ee": ("sbuf", [128, 2 * NS], "float32"), "aa": ("sbuf", [128, 2 * NS], "float32"), "tt": ("sbuf", [128, 2 * NS], "float32"),
+    "yy": ("sbuf", [128, 2 * NS], "float32"), "zz": ("sbuf", [128, 2 * NS], "float32"), "z2": ("sbuf", [128, 2 * NS], "float32"),
     "dd": ("sbuf", [128, 2 * NS], "float32"), "fd": ("sbuf", [128, 2 * NS], "float32"),
-    "of": ("sbuf", [128, 4 * NS], "float32"), "oa": ("sbuf", [128, 2 * NS], "uint16"), "oc": ("sbuf", [128, 2 * NS], "uint16"),
+    "of": ("sbuf", [128, 4, NS], "float32"),
+    "o1": ("sbuf", [128, 9, 16], "uint16"), "o2": ("sbuf", [128, 6, 8], "uint16"), "od": ("sbuf", [128, NS], "uint16"),
     "pl": ("sbuf", [128, 32], "int32"), "pz": ("sbuf", [128, 16], "int32"), "pu": ("sbuf", [128, 32], "uint16"),
     "zu": ("sbuf", [128, 400], "float32"), "zv": ("sbuf", [128, 384], "float32"),
     "gu": ("sbuf", [128, P], "float32"), "yb": ("sbuf", [128, P], "float32"),
     "zp": ("psum", [128, 2048], "float32"), "pp": ("psum", [128, 2048], "float32"),
 }
-for (_i, _h), _w in WORK.items():
-    SCRATCH["g%d%s" % (_i, _h)] = ("sbuf", [128, _w * CH[_h][1]], "bfloat16")
-    SCRATCH["s%d%s" % (_i, _h)] = ("sbuf", [128, _w * CH[_h][1]], "bfloat16")
-SEMAPHORES = ["cv", "cs_", "ct", "cg", "lists", "x0", "x1", "a0", "a1", "a2", "uv", "pfg", "y0", "y1", "arr0", "arr1", "sent"]
-
-
-def order(q):
-    return [(q + 1 + k) % N for k in range(N)]
-
-
-def places(r):
-    return [(r + 3 + k) % N for k in range(3)] + [(r + 1 + k) % N for k in range(2)]
-
-
-def runs(ranks):
-    out = []
-    for k, q in enumerate(ranks):
-        if out and out[-1][1] + out[-1][2] == q:
-            out[-1][2] += 1
-        else:
-            out.append([k, q, 1])
-    return out
-
-
-def sending(q, T, topo):
-    out = []
-    for ds in (order(q)[0:3], order(q)[3:5]):
-        eng = topo.engines(T.cores[q], T.cores[ds[0]])
-        ev, od = eng[0::2], eng[1::2]
-        k = len(ev) // 2
-        ds = sorted(ds, key=lambda r: topo.die(T.cores[r]) == topo.die(T.cores[q]))
-        es = ([ev[:k], ev[k:], od], [od[:k], od[k:], ev]) if len(ds) == 3 else ([ev, od], [od, ev])
-        out.append([[(r, e) for r, e in zip(ds, x)] for x in es])
-    return out
+for (_h, _p), _w in WORK.items():
+    SCRATCH["g%s%d" % (_h, _p)] = ("sbuf", [128, 2 * _w * CH[_h][1]], "bfloat16")
+    SCRATCH["s%s%d" % (_h, _p)] = ("sbuf", [128, 2 * _w * CH[_h][1]], "bfloat16")
+    SCRATCH["c%s%d" % (_h, _p)] = ("sbuf", [128, 2 * CH[_h][1]], "bfloat16")
+SEMAPHORES = ["cv", "cs_", "ct", "cg", "lists", "x0", "x1", "a0", "a1", "a2", "a3", "uv", "pfg", "y0", "y1", "arr0", "arr1", "arr2", "sent"]
 
 
 def rank_program(g, core, T, topo):
@@ -93,6 +66,9 @@ def rank_program(g, core, T, topo):
     count = {k: 0 for k in que}
     seen = {k: {} for k in que}
     v, s, t = g.vector, g.scalar, g.tensor
+    pair, mate = rank // 2, rank ^ 1
+    to = {"a": (pair + 1) % 3, "b": (pair + 2) % 3}
+    frm = [(pair + 2) % 3, (pair + 1) % 3]
 
     def need(q, *toks):
         for sem, val in toks:
@@ -105,26 +81,26 @@ def rank_program(g, core, T, topo):
         count[q] += 1
         return (q, count[q])
 
-    s.dma_start(T.ll[:, NS:2 * NS], T.ln[:]).then_inc(T.sem.lists, 16)
-    g.sync.dma_start(T.ll[:, 0:NS], T.lo[:]).then_inc(T.sem.lists, 16)
+    s.dma_start(T.ll[:, 0:NS], T.ln[:]).then_inc(T.sem.lists, 16)
+    g.sync.dma_start(T.ll[:, 2 * NS:3 * NS], T.lo[:]).then_inc(T.sem.lists, 16)
     g.sync.dma_start(T.xb[:, 0:4 * XC], T.x[:, 0:4 * XC]).then_inc(T.sem.x0, 16)
     s.dma_start(T.ab[:, 0:512], T.a[:, 0:512]).then_inc(T.sem.a0, 16)
     g.sync.dma_start(T.xb[:, 4 * XC:2048], T.x[:, 4 * XC:2048]).then_inc(T.sem.x1, 16)
-    g.sync.dma_start(T.ab[:, 512:1024], T.a[:, 512:1024]).then_inc(T.sem.a1, 16)
-    g.sync.dma_start(T.ab[:, 1024:2048], T.a[:, 1024:2048]).then_inc(T.sem.a2, 16)
+    for i in (1, 2, 3):
+        g.sync.dma_start(T.ab[:, 512 * i:512 * i + 512], T.a[:, 512 * i:512 * i + 512]).then_inc(T.sem["a%d" % i], 16)
     g.sync.dma_start(T.ub[:], T.u[:]).then_inc(T.sem.uv, 16)
     g.sync.dma_start(T.vb[:], T.v[:]).then_inc(T.sem.uv, 16)
     for k in range(8):
         g.sync.dma_start(T.pl[16 * k:16 * k + 16, 0:16], T.pf[:]).then_inc(T.sem.pfg, 16)
         g.sync.dma_start(T.pl[16 * k:16 * k + 16, 16:32], T.pg[:]).then_inc(T.sem.pfg, 16)
 
+    def at(i):
+        return (i // 2) * RG + (i % 2) * ST
+
     k_one = done("cv", v.memset(T.ones[:], 1.0))
-    k_mo = done("cv", v.memset(T.mc[:, 3 * 2 * NB:6 * 2 * NB], 1.0))
-    k_aw = done("cv", v.memset(T.aw[:], 1.0))
+    for i in range(4):
+        k_hp = done("cv", v.memset(T.win[:, at(i) + H0 + T_COLS:at(i) + H0 + ST], 0.0))
     k_zu = done("cv", v.memset(T.zu[:, 384:400], 0.0))
-    need("cv", k_aw)
-    done("cv", v.memset(T.aw[:, 0::LV], 0.0))
-    k_aw = done("cv", v.memset(T.aw[:, 1::LV], float(W)))
 
     need("cg", k_one)
 
@@ -132,264 +108,269 @@ def rank_program(g, core, T, topo):
         return done("cg", g.affine_select(out, T.ones[:, 0:n], [[0, n // b], [1, b]], A.is_gt, 0.0, 0, 0))
 
     k_m6 = mask(T.m6[:], ST, B)
-    for m in range(1, 4):
-        k_mc = mask(T.mc[:, 2 * NB * (m - 1):2 * NB * m], 2 * NB, 1 << m)
-    k_ms = {3: mask(T.m3[:], 960, 3)}
-    if 2 in WORK.values():
-        k_ms[2] = mask(T.m2[:], 640, 2)
-
-    def zero(out, n):
-        return done("cs_", s.activation(out, T.ones[:, 0:n], F.Copy, scale=0.0))
+    k_ms = {2: mask(T.m2[:], 512, 2), 3: mask(T.m3[:], 384, 3)}
 
     need("cs_", k_one)
-    for i in range(4):
-        b = (i // 2) * RG + (i % 2) * ST
-        k_hp = zero(T.win[:, b + T_COLS:b + ST], ST - T_COLS)
+    lead, tail = E0 + shift(LV), E0 + shift(LV) + B * (NB + USED - 2 ** LV) + 1
     for p in range(2):
-        zero(T.win[:, p * RG + 6 * ST:p * RG + EP + LV], EP + LV - 6 * ST)
-        zero(T.win[:, p * RG + ES + 2 * ST - LV:p * RG + RG], LV)
-    need("cs_", k_mo)
-    for m in range(4, 7):
-        for p in range(2):
-            b = 2 * NB * (m - 1) + NB * p
-            k_mz = zero(T.mc[:, b:b + NB:1 << m], len(range(0, NB, 1 << m)))
+        for a, b in ((P0 + J, lead), (tail, RG)):
+            k_ez = done("cs_", s.activation(T.win[:, p * RG + a:p * RG + b], T.ones[:, 0:b - a], F.Copy, scale=0.0))
 
-    c = CC * ((rank + 1) % N)
-    cuts = [(0, c, NS - c)] + ([(NS - c, 0, c)] if c else [])
-    need("cv", ("lists", 32))
-    for o, b, n in cuts:
-        done("cv", v.tensor_copy(T.ld[:, NS + o:NS + o + n], T.ll[:, b:b + n]))
-    for o, b, n in cuts:
-        k_lm = done("cv", v.tensor_scalar(T.lm[:, o:o + n], T.ll[:, NS + b:NS + b + n], -1, None, A.add))
-    LR = T.ld[:, NS:3 * NS]
-    need("cv", k_lm)
-    k = done("cv", v.tensor_tensor(T.ld[:, 2 * NS:3 * NS], T.ld[:, NS:2 * NS], T.lm[:], A.add))
-    need("cv", k)
-    k = done("cv", v.tensor_scalar(T.l6[:], LR, 171, None, A.mult))
-    need("cs_", k_lm)
-    done("cs_", s.activation(T.ee[:, 0:NS], T.lm[:], F.Sign))
-    k_ee = done("cs_", s.activation(T.ee[:, NS:2 * NS], T.lm[:], F.Sign, scale=-1.0))
-    need("cv", k)
-    k = done("cv", v.tensor_scalar(T.sb[:], T.l6[:], 10, None, A.arith_shift_right))
-    for j in range(3):
-        done("cv", v.tensor_scalar(T.sh[:, j::LV], T.l6[:], 11 + j, None, A.arith_shift_right))
-    need("cv", k)
-    done("cv", v.tensor_scalar(T.ld[:, 0:NS], T.sb[:, 0:NS], B, CE, A.mult, A.add))
-    k_ld = done("cv", v.tensor_scalar(T.ld[:, 3 * NS:4 * NS], T.sb[:, NS:2 * NS], B, DE, A.mult, A.add))
+    def vec(call, *args, deps=()):
+        need("cv", *deps)
+        return done("cv", call(*args))
+
+    def act(out, src, f, scale, *deps):
+        need("cs_", *deps)
+        return done("cs_", s.activation(out, src, f, scale=scale))
+
+    ts, tt = v.tensor_scalar, v.tensor_tensor
+    lo_, hi_ = slice(0, NS), slice(NS, 2 * NS)
+    n_, L_, R_, LR, RL = T.ll[:, lo_], T.ll[:, 2 * NS:3 * NS], T.ll[:, 3 * NS:4 * NS], T.ll[:, 2 * NS:4 * NS], T.ll[:, NS:3 * NS]
+    lm_, r1_, nb_, q_, q2_, w_ = (T.qq[:, k * NS:(k + 1) * NS] for k in range(6))
+    todo = [
+        ("r1", "in", tt, r1_, L_, n_, A.add),
+        ("lm", "in", ts, lm_, n_, -1, None, A.add),
+        ("l6", "in", ts, T.l6[:, lo_], L_, B, 683, A.add, A.mult),
+        ("e", "in", ts, T.ee[:, lo_], n_, -1, 1, A.add, A.min),
+        ("r6", "r1", ts, T.l6[:, hi_], r1_, -1, 683, A.add, A.mult),
+        ("r", "lm", tt, R_, L_, lm_, A.add),
+        ("r2", "r1", ts, T.ll[:, hi_], r1_, 1, None, A.add),
+        ("ne", "lm", ts, T.ee[:, hi_], lm_, -1, -1, A.mult, A.max),
+        ("sb", "r6", ts, T.sb[:], T.l6[:], 12, None, A.arith_shift_right),
+        ("yy", "ne", tt, T.yy[:], LR, T.ee[:], A.add),
+        ("nb", "sb", tt, nb_, T.sb[:, hi_], T.sb[:, lo_], A.subtract),
+        ("b6", "sb", ts, T.b6[:], T.sb[:], B, -B - 0.25, A.mult, A.add),
+        ("q", "nb", ts, q_, nb_, PHI, None, A.mult),
+        ("q2", "nb", ts, q2_, nb_, PHI, LESS, A.mult, A.mult),
+        ("tc", "nb", ts, T.tt[:, lo_], nb_, 2, K, A.min, A.mult),
+        ("td", "nb", ts, T.tt[:, hi_], nb_, 2, K, A.min, A.mult),
+        ("dd", "b6", tt, T.dd[:], T.b6[:], RL, A.subtract),
+        ("w", "q2", tt, w_, q_, q2_, A.subtract),
+        ("zz", "td", tt, T.zz[:], T.b6[:], T.tt[:], A.add),
+        ("fd", "dd", ts, T.fd[:], T.dd[:], -B - 0.5, J, A.is_ge, A.mult),
+        ("ac", "w", ts, T.aa[:, lo_], w_, 0, 1 / 3, A.max, A.mult),
+        ("ad", "w", ts, T.aa[:, hi_], w_, 0, 1 / 3 - B, A.max, A.mult),
+        ("z2", "zz", tt, T.z2[:], T.zz[:], T.yy[:], A.max),
+        ("ab", "fd", tt, T.of[:, 0:2, :], LR, T.fd[:], A.add),
+        ("of", "z2", tt, T.of[:, 2:4, :], T.z2[:], T.aa[:], A.add),
+        ("o0", "of", ts, T.o1[:, :, 0:8], T.of[:, 0:3, :], 0, None, A.add),
+        ("o1", "of", ts, T.o1[:, :, 8:16], T.of[:, 0:3, :], ST, None, A.add),
+        ("od", "of", v.tensor_copy, T.od[:], T.of[:, 3, :]),
+        ("o2", "of", ts, T.o2[:, :, 0:4], T.of[:, 0:3, 8 * pair:8 * pair + 8], 0, None, A.add),
+        ("o3", "of", ts, T.o2[:, :, 4:8], T.of[:, 0:3, 8 * pair:8 * pair + 8], ST, None, A.add),
+    ]
+    made = {"in": ("lists", 32)}
+
+    def lists(upto):
+        while upto not in made:
+            name, reads, *call = todo[len(made) - 1]
+            made[name] = vec(*call, deps=[made[reads]])
 
     def quant(out, sc, src, *deps):
         need("cv", *deps)
         return done("cv", v.quantize_mx(out, sc, src))
 
-    k_x0 = quant(T.xq[:, 0:XC], T.xs[:, 0:XC], T.xb[:, 0:4 * XC], ("x0", 16))
-    need("cv", k_ld)
-    k = done("cv", v.tensor_tensor(T.dd[:], T.ld[:, 0:2 * NS], T.ld[:, 2 * NS:4 * NS], A.subtract))
-    k_a = [quant(T.aq[:, 0:128], T.sa[:, 0:128], T.ab[:, 0:512], ("a0", 16))]
-    need("cv", k)
-    done("cv", v.tensor_scalar(T.fd[:, 0:NS], T.dd[:, 0:NS], CE - (B - 1), S6, A.is_le, A.mult))
-    k = done("cv", v.tensor_scalar(T.fd[:, NS:2 * NS], T.dd[:, NS:2 * NS], -DE, P6, A.is_le, A.mult))
-    for j in range(3, LV):
-        k_sh = done("cv", v.tensor_scalar(T.sh[:, j::LV], T.l6[:], 11 + j, None, A.arith_shift_right))
-    need("cv", k)
-    k = done("cv", v.tensor_tensor(T.of[:, 0:2 * NS], LR, T.fd[:], A.add))
-    k_x1 = quant(T.xq[:, XC:512], T.xs[:, XC:512], T.xb[:, 4 * XC:2048], ("x1", 16))
-    need("cv", k)
-    k_oa = done("cv", v.tensor_copy(T.oa[:], T.of[:, 0:2 * NS]))
-
-    def levels():
-        need("cv", k_sh)
-        return done("cv", v.tensor_tensor(T.fl[:], T.sh[:, 0:LV * NS], T.sh[:, LV * NS:2 * LV * NS], A.not_equal))
-
-    def offsets(k):
-        need("cv", k, k_aw)
-        k = done("cv", v.tensor_tensor_scan(T.cn[:], T.aw[:], T.fl[:], 0.0, A.mult, A.add))
-        need("cv", k_ee)
-        done("cv", v.tensor_tensor(T.yy[:], LR, T.ee[:], A.add))
-        need("cv", k)
-        done("cv", v.tensor_tensor(T.xm[:, 0:NS], T.ld[:, 0:NS], T.cn[:, LV - 1::LV], A.add))
-        k = done("cv", v.tensor_tensor(T.xm[:, NS:2 * NS], T.ld[:, 3 * NS:4 * NS], T.cn[:, LV - 1::LV], A.add))
-        need("cv", k)
-        k = done("cv", v.tensor_tensor(T.of[:, 2 * NS:4 * NS], T.xm[:], T.yy[:], A.max))
-        need("cv", k)
-        return done("cv", v.tensor_copy(T.oc[:], T.of[:, 2 * NS:4 * NS]))
+    def quant_a(i):
+        return quant(T.aq[:, 128 * i:128 * i + 128], T.sa[:, 128 * i:128 * i + 128], T.ab[:, 512 * i:512 * i + 512], ("a%d" % i, 16))
 
     def mm(out, w, ws, x, xs, *deps):
         need("ct", *deps)
         return done("ct", t.matmul_mx(out, w, ws, x, xs, True, True))
 
-    def at(i):
-        return (i // 2) * RG + (i % 2) * ST
+    k_h = {}
 
-    def relu(i, c, n, src, *deps):
-        need("cs_", *deps)
-        return done("cs_", s.activation(T.win[:, at(i) + c:at(i) + c + n], src, F.Relu, scale=0.05))
+    def bank(k, a, b):
+        return T.zp[:, 512 * k + a:512 * k + b] if k < 4 else T.pp[:, 512 * (k - 4) + a:512 * (k - 4) + b]
 
-    k0 = mm(T.zp[:, 0:XC], T.aq[:, 0:128], T.sa[:, 0:128], T.xq[:, 0:XC], T.xs[:, 0:XC], k_x0, k_a[0])
-    k1 = mm(T.pp[:, 1536:2048 - XC], T.aq[:, 0:128], T.sa[:, 0:128], T.xq[:, XC:512], T.xs[:, XC:512], k_x1)
-    k_h = {0: relu(0, 0, XC, T.zp[:, 0:XC], k0), 4: relu(0, XC, 512 - XC, T.pp[:, 1536:2048 - XC], k1)}
+    def product(i, a, b, ps, *deps):
+        k = mm(bank(ps, 0, b - a), T.aq[:, 128 * i:128 * i + 128], T.sa[:, 128 * i:128 * i + 128], T.xq[:, a:b], T.xs[:, a:b], *deps)
+        k_h[i, a] = act(T.win[:, at(i) + H0 + a:at(i) + H0 + b], bank(ps, 0, b - a), F.Relu, 0.05, k)
 
-    def product(i):
-        return mm(T.zp[:, 512 * i:512 * i + 512], T.aq[:, 128 * i:128 * i + 128], T.sa[:, 128 * i:128 * i + 128], T.xq[:], T.xs[:], k_a[i])
-
-    def empty(i, k):
-        k_h[i] = relu(i, 0, 512, T.zp[:, 512 * i:512 * i + 512], k)
+    scan = v.tensor_tensor_scan
 
     def prefix(i, a, b, *deps):
         w = at(i)
-        need("cv", k_m6, k_hp, *deps)
-        return done("cv", v.tensor_tensor_scan(T.win[:, w + P6 + a:w + P6 + b], T.m6[:, a:b], T.win[:, w + a:w + b], 0.0, A.mult, A.max))
+        return vec(scan, T.win[:, w + P0 + a:w + P0 + b], T.m6[:, a:b], T.win[:, w + H0 + a:w + H0 + b], 0.0, A.mult, A.max, deps=(k_m6, k_hp) + deps)
 
     def suffix(i, *deps):
         w = at(i)
-        need("cv", k_m6, k_hp, *deps)
-        end = w - 1 if w else None
-        return done("cv", v.tensor_tensor_scan(T.win[:, w + S6 + ST - 1:w + S6 - 1:-1], T.m6[:], T.win[:, w + ST - 1:end:-1], 0.0, A.mult, A.max))
+        end = w + S0 - 1 if w + S0 else None
+        return vec(scan, T.win[:, w + S0 + ST - 1:end:-1], T.m6[:], T.win[:, w + H0 + ST - 1:w + H0 - 1:-1], 0.0, A.mult, A.max, deps=(k_m6, k_hp) + deps)
 
-    def coarse(p, k_p):
-        b, n = p * RG, 2 * NB
-        need("cv", k_mc, k_mz, k_p)
-        for m in range(1, 7):
-            o = n * (m - 1)
-            done("cv", v.tensor_tensor_scan(T.win[:, b + EP + LV + m - 1:b + EP + 2 * ST:LV], T.win[:, b + P6 + B - 1:b + P6 + 2 * ST - B:B],
-                                            T.mc[:, o + 1:o + n], 0.0, A.max, A.mult))
-            tok = done("cv", v.tensor_tensor_scan(T.win[:, b + ES + LV * (n - 2) + m - 1:b + ES - 1:-LV], T.win[:, b + P6 + 2 * ST - 1:b + P6 + B:-B],
-                                                  T.mc[:, o + n - 1:o:-1], 0.0, A.max, A.mult))
-        return tok
+    k_e = {}
 
-    WIN = [S6 + ST, P6 + ST, ES + ST, EP + ST]
+    def level(p, m, *deps):
+        n = NB + USED + 1 - 2 ** m
+        a = p * RG + (E0 + shift(m - 1) if m > 1 else P0 + B - 1)
+        b, o = a + B * 2 ** (m - 1), p * RG + E0 + shift(m)
+        k_e[p] = vec(scan, T.win[:, o:o + B * (n - 1) + 1:B], T.win[:, a:a + B * (n - 1) + 1:B], T.win[:, b:b + B * (n - 1) + 1:B],
+                     BIG, A.min, A.max, deps=(k_ez, k_e[p]))
 
-    def part(i, e, c, n):
-        o = (e % 2) * NS + c // 16
-        return T.win[:, at(i):at(i) + WIN[e]].indirect((T.oa if e < 2 else T.oc)[:, o:o + n // 16])
+    WIN = [(S0, P0), (H0, P0 + J), (H0, RG)]
 
-    tok = {}
+    def part(h, p, e, js=(0, 2)):
+        a, b = WIN[e]
+        if h in to:
+            off = T.o1[:, 3 * e + to[h], 8 * js[0]:8 * js[1]]
+        else:
+            off = T.o2[:, 2 * e + (mate if h == "m" else rank) % 2, 4 * js[0]:4 * js[1]]
+        return T.win[:, p * RG + a:p * RG + b].indirect(off)
 
-    def gather(i, h, es, *deps):
-        w, (c, n) = WORK[i, h], CH[h]
+    got, k_s, k_t = {}, {}, {}
+
+    def gather(h, p, es, *deps):
+        w, n = WORK[h, p], 2 * CH[h][1]
         for e in es:
             if e < w:
                 need("cs_", *deps)
-                tok[i, h] = done("cs_", s.activation(T["g%d%s" % (i, h)][:, e:w * n:w], part(i, e, c, n), F.Copy))
+                got[h, p] = done("cs_", s.activation(T["g%s%d" % (h, p)][:, e:w * n:w], part(h, p, e), F.Copy))
 
-    def best(i, h):
-        w, (c, n) = WORK[i, h], CH[h]
-        need("cv", k_ms[w], tok[i, h])
-        msk, src, dst = T["m%d" % w], T["g%d%s" % (i, h)], T["s%d%s" % (i, h)]
-        k = done("cv", v.tensor_tensor_scan(dst[:, 0:w * n], msk[:, 0:w * n], src[:, 0:w * n], 0.0, A.mult, A.max))
-        if w == 2:
-            need("cv", k)
-            k = done("cv", v.tensor_tensor(src[:, 0:n], part(i, 2, c, n), dst[:, 1:2 * n:2], A.max))
-        return k
+    def best(h, p, *js):
+        w = WORK[h, p]
+        a, b = w * CH[h][1] * js[0], w * CH[h][1] * (js[-1] + 1)
+        k = vec(scan, T["s%s%d" % (h, p)][:, a:b], T["m%d" % w][:, 0:b - a], T["g%s%d" % (h, p)][:, a:b], 0.0, A.mult, A.max, deps=[k_ms[w], got[h, p]])
+        for j in js:
+            k_s[h, p, j] = k
 
-    def last(i, h, k):
-        w, (c, n) = WORK[i, h], CH[h]
-        need("cv", k)
-        cur = T["s%d%s" % (i, h)][:, 2:3 * n:3] if w == 3 else T["g%d%s" % (i, h)][:, 0:n]
-        return done("cv", v.tensor_tensor(T.tile[:, 4 * c + i:4 * (c + n):4], part(i, 3, c, n), cur, A.max))
+    def third(h, p, *js):
+        a, b = CH[h][1] * js[0], CH[h][1] * (js[-1] + 1)
+        k = vec(tt, T["c%s%d" % (h, p)][:, a:b], part(h, p, 2, (js[0], js[-1] + 1)), T["s%s%d" % (h, p)][:, 2 * a + 1:2 * b:2], A.max,
+                deps=[k_e[p], k_s[h, p, js[-1]]])
+        for j in js:
+            k_s[h, p, j] = k
 
-    def merge(*todo):
-        b = best(*todo[0])
-        for j, x in enumerate(todo):
-            n = best(*todo[j + 1]) if j + 1 < len(todo) else None
-            k = last(*x, b)
-            b = n
-        return k
+    def last(h, p, j):
+        w, (c, n) = WORK[h, p], CH[h]
+        o = 8 * to[h] if h in to else 4 * (mate if h == "m" else rank)
+        cur = T["s%s%d" % (h, p)][:, 3 * n * j + 2:3 * n * (j + 1):3] if w == 3 else T["c%s%d" % (h, p)][:, n * j:n * (j + 1)]
+        src = T.win[:, at(2 * p + j) + H0:p * RG + RG].indirect(T.od[:, o:o + n // 16])
+        k_t[h] = vec(tt, T.tile[:, 4 * c + 2 * p + j:4 * (c + n):4], src, cur, A.max, deps=[made["od"], k_s[h, p, j]])
 
-    def pack(c, n, k):
-        return quant(T.cq[:, c:c + n], T.cs[:, c:c + n], T.tile[:, 4 * c:4 * (c + n)], k)
+    k_c = {}
 
-    prefix(0, 0, XC, k_h[0])
-    k_a.append(quant(T.aq[:, 128:256], T.sa[:, 128:256], T.ab[:, 512:1024], ("a1", 16)))
-    empty(1, product(1))
-    k_f = levels()
-    ks0 = suffix(0, k_h[4])
+    def pack(h):
+        c, o = {"a": (0, 128), "b": (128, 256), "m": (192, 0)}[h]
+        k_c[h] = quant(T.cq[:, o:o + 128], T.cs[:, o:o + 128], T.tile[:, 4 * c:4 * c + 512], k_t[h])
+
+    lists("b6")
+    k_x0 = quant(T.xq[:, 0:XC], T.xs[:, 0:XC], T.xb[:, 0:4 * XC], ("x0", 16))
+    product(0, 0, XC, 0, k_x0, quant_a(0))
+    lists("dd")
+    k_x1 = quant(T.xq[:, XC:512], T.xs[:, XC:512], T.xb[:, 4 * XC:2048], ("x1", 16))
+    product(0, XC, 512, 7, k_x1)
+    lists("fd")
+    product(1, 0, XC, 1, quant_a(1))
+    product(1, XC, 512, 6)
+    prefix(0, 0, XC, k_h[0, 0])
+    lists("ab")
+    product(2, 0, 512, 2, quant_a(2))
+    lists("of")
+    suffix(0, k_h[0, XC])
+    product(3, 0, 512, 3, quant_a(3))
     prefix(0, XC, ST)
-    k_oc = offsets(k_f)
-    k_a.append(quant(T.aq[:, 256:512], T.sa[:, 256:512], T.ab[:, 1024:2048], ("a2", 16)))
-    k_a.append(k_a[2])
-    z2, z3 = product(2), product(3)
-    ks1 = suffix(1, k_h[1])
-    kp1 = prefix(1, 0, ST)
-    t01 = coarse(0, kp1)
-    gather(0, "a", (0,), k_oa, ks0, k_h[1])
-    gather(0, "a", (1,), ks1)
-    empty(2, z2)
-    empty(3, z3)
-    gather(1, "f", (0, 1), kp1)
-    gather(0, "a", (2,), k_oc, t01)
-    gather(1, "f", (2,))
-    ks2, kp2 = suffix(2, k_h[2]), prefix(2, 0, ST)
-    ks3, kp3 = suffix(3, k_h[3]), prefix(3, 0, ST)
-    t23 = coarse(1, kp3)
-    gather(2, "f", (0, 1), ks3)
-    gather(3, "f", (0, 1), kp3)
-    for i, h in ((2, "f"), (3, "f")):
-        gather(i, h, (2,), t23)
-    for i, h in ((1, "n"), (2, "n"), (3, "n"), (0, "o"), (1, "o"), (2, "o"), (3, "o")):
-        gather(i, h, (0, 1, 2))
-    merge((0, "a"))
-    k_c0 = pack(0, FAR, merge((1, "f"), (2, "f"), (3, "f")))
-    k_c1 = pack(FAR, NEAR, merge((1, "n"), (2, "n"), (3, "n")))
-
-    sent = 0
-    for h, (k, half) in enumerate(zip((k_c0, k_c1), sending(rank, T, topo))):
-        need("cg", k)
-        for what in (0, 1):
-            trs = []
-            for r, es in half[what]:
-                rid, pnc = topo.addr(T.cores[r])[0:2]
-                msk = 0
-                for e in es:
-                    msk |= 1 << e
-                a, b = CAPP * order(rank).index(r), CAPP * places(r).index(rank)
-                if what == 0:
-                    src, out = T.cq[:, a:a + CAPP].bitcast(dt.uint8), T.rq[:, b:b + CAPP].bitcast(dt.uint8)
-                else:
-                    src, out = T.cs[:, a:a + CAPP], T.rs[:, b:b + CAPP]
-                trs.append(RemoteDMATransfer(dst_ids=[DstId(rid=rid, pnc=pnc)], dma_engine_mask=msk, remote_sem=T.sem["arr%d" % h], src=src, dst=out))
-                sent += len(es)
-            g.remote_dma_fused(trs, local_sem=T.sem.sent)
-    arrive = [0, 0]
-    for q in range(N):
-        if q != rank:
-            for h, half in enumerate(sending(q, T, topo)):
-                for what in half:
-                    arrive[h] += sum(len(es) for r, es in what if r == rank)
-
+    lists("o1")
+    k_e[0] = prefix(1, 0, ST, k_h[1, XC])
+    gather("a", 0, (0, 1), made["o1"], suffix(1))
+    level(0, 1)
+    suffix(2, k_h[2, 0])
+    level(0, 2)
+    prefix(2, 0, ST)
+    level(0, 3)
+    k_e[1] = prefix(3, 0, ST, k_h[3, 0])
+    level(0, 4)
+    gather("a", 1, (0, 1), suffix(3))
+    level(0, 5)
+    level(1, 1)
+    lists("o3")
+    level(0, 6)
+    gather("b", 0, (0, 1, 2), k_e[0])
+    level(1, 2)
+    best("a", 0, 0, 1)
+    level(1, 3)
+    third("a", 0, 0)
+    level(1, 4)
+    third("a", 0, 1)
+    level(1, 5)
+    last("a", 0, 0)
+    level(1, 6)
+    gather("b", 1, (0, 1, 2), k_e[1])
+    for h in "mo":
+        for p in range(2):
+            gather(h, p, (0, 1, 2), made["o3"])
+    best("a", 1, 0, 1)
+    last("a", 0, 1)
     k_u = quant(T.uq[:], T.us[:], T.ub[:], ("uv", 32))
     k_v = quant(T.vq[:], T.vs[:], T.vb[:], ("uv", 32))
-    need("cv", ("pfg", 256))
-    k = done("cv", v.tensor_scalar(T.pz[:], T.pl[:, 16:32], 0, SL, A.is_lt, A.mult))
-    merge((0, "o"))
-    need("cv", k)
-    k = done("cv", v.tensor_tensor(T.pl[:, 16:32], T.pl[:, 16:32], T.pz[:], A.max))
-    merge((1, "o"))
-    need("cv", k)
-    k_pu = done("cv", v.tensor_copy(T.pu[:], T.pl[:]))
-    k_co = quant(T.oq[:], T.ow[:], T.tile[:, 4 * (SL - 128):4 * SL], merge((2, "o"), (3, "o")))
+    third("a", 1, 0)
+    third("a", 1, 1)
+    last("a", 1, 0)
+    last("a", 1, 1)
+    best("b", 0, 0)
+    best("b", 0, 1)
+    pack("a")
+    last("b", 0, 0)
+    last("b", 0, 1)
+    best("b", 1, 0)
+    best("b", 1, 1)
+    last("b", 1, 0)
+    last("b", 1, 1)
+    best("m", 0, 0, 1)
+    pack("b")
+    last("m", 0, 0)
+    best("m", 1, 0, 1)
+    last("m", 0, 1)
+    last("m", 1, 0)
+    last("m", 1, 1)
+    best("o", 0, 0, 1)
+    pack("m")
 
-    ku = mm(T.pp[:, 0:FAR], T.uq[:], T.us[:], T.rq[:, 0:FAR], T.rs[:, 0:FAR], k_u, k_v, ("arr0", arrive[0]))
-    kv = mm(T.pp[:, 512:512 + FAR], T.vq[:], T.vs[:], T.rq[:, 0:FAR], T.rs[:, 0:FAR])
-    kuo = mm(T.pp[:, 1024:1152], T.uq[:], T.us[:], T.oq[:], T.ow[:], k_co)
-    kvo = mm(T.pp[:, 1536:1664], T.vq[:], T.vs[:], T.oq[:], T.ow[:])
+    def transfer(r, es, src, out, h):
+        rid, pnc = topo.addr(T.cores[r])[0:2]
+        return RemoteDMATransfer(dst_ids=[DstId(rid=rid, pnc=pnc)], dma_engine_mask=sum(1 << e for e in es), remote_sem=T.sem["arr%d" % h], src=src, dst=out)
 
-    def natural(q, out, src, ranks, c, k):
-        need(q, k)
-        for o, r, n in runs(ranks):
-            d, x = out[:, CAPP * r:CAPP * (r + n)], src[:, c + CAPP * o:c + CAPP * (o + n)]
-            tok = done(q, s.activation(d, x, F.Copy) if q == "cs_" else v.tensor_copy(d, x))
-        return tok
+    eng = topo.engines(core, T.cores[mate])
+    half = [eng[0::2], eng[1::2]]
+    for h in range(2):
+        need("cg", k_c["ab"[h]])
+        a, b = 128 * h + 128, 128 * h + CAPP * (rank % 2)
+        ds = [(2 * to["ab"[h]] + j, a + CAPP * j) for j in range(2)]
+        g.remote_dma_fused([transfer(r, half[j], T.cq[:, c:c + CAPP].bitcast(dt.uint8), T.rq[:, b:b + CAPP].bitcast(dt.uint8), h)
+                            for j, (r, c) in enumerate(ds)], local_sem=T.sem.sent)
+        g.remote_dma_fused([transfer(r, half[j], T.cs[:, c:c + CAPP], T.rs[:, b:b + CAPP], h) for j, (r, c) in enumerate(ds)], local_sem=T.sem.sent)
+    need("cg", k_c["m"])
+    g.remote_dma_fused([transfer(mate, half[0], T.cq[:, CAPP:128].bitcast(dt.uint8), T.rq[:, 256:320].bitcast(dt.uint8), 2),
+                        transfer(mate, half[1], T.cs[:, CAPP:CAPP + 256], T.rs[:, 256:512], 2)], local_sem=T.sem.sent)
+    sent, arrive = 5 * len(eng), [2 * len(eng), 2 * len(eng), len(eng)]
 
-    far, near = places(rank)[0:3], places(rank)[3:5]
-    natural("cs_", T.zu, T.pp, far, 0, ku)
-    natural("cv", T.zv, T.pp, far, 512, kv)
-    natural("cs_", T.zu, T.pp, [rank], 1024 + 128 - CAPP, kuo)
-    natural("cv", T.zv, T.pp, [rank], 1536 + 128 - CAPP, kvo)
+    def both(c, x, xs, *deps):
+        return [(c + j, mm(bank(c + j, 0, 128), w[:], ws[:], x, xs, *deps)) for j, (w, ws) in enumerate(((T.uq, T.us), (T.vq, T.vs)))]
 
-    ku = mm(T.zp[:, 0:NEAR], T.uq[:], T.us[:], T.rq[:, FAR:320], T.rs[:, FAR:320], ("arr1", arrive[1]))
-    kv = mm(T.zp[:, 512:512 + NEAR], T.vq[:], T.vs[:], T.rq[:, FAR:320], T.rs[:, FAR:320])
-    k_zu2 = natural("cs_", T.zu, T.zp, near, 0, ku)
-    k_zv = natural("cv", T.zv, T.zp, near, 512, kv)
+    def natural(ks, c, o, n, split):
+        (bu, ku), (bv, kv) = ks
+        ku = act(T.zu[:, o:o + n], bank(bu, c, c + n), F.Copy, 1.0, ku)
+        if split:
+            return ku, vec(v.tensor_copy, T.zv[:, o:o + n], bank(bv, c, c + n), deps=[kv])
+        return ku, act(T.zv[:, o:o + n], bank(bv, c, c + n), F.Copy, 1.0, kv)
+
+    p0 = both(4, T.rq[:, 0:128], T.rs[:, 0:128], k_u, k_v, ("arr0", arrive[0]))
+    p1 = both(6, T.rq[:, 128:256], T.rs[:, 128:256], ("arr1", arrive[1]))
+    best("o", 1, 0, 1)
+    last("o", 0, 0)
+    last("o", 0, 1)
+    last("o", 1, 0)
+    last("o", 1, 1)
+    k = vec(ts, T.pz[:], T.pl[:, 16:32], 0, SL, A.is_lt, A.mult, deps=[("pfg", 256)])
+    k_co = quant(T.oq[:], T.ow[:], T.tile[:, 4 * (SL - 128):4 * SL], k_t["o"])
+    k = vec(tt, T.pl[:, 16:32], T.pl[:, 16:32], T.pz[:], A.max, deps=[k])
+    k_pu = vec(v.tensor_copy, T.pu[:], T.pl[:], deps=[k])
+    po = both(0, T.oq[:], T.ow[:], k_co)
+    pm = both(2, T.rq[:, 192:320], T.rs[:, 192:320], ("arr2", arrive[2]))
+    natural(p0, 0, 128 * frm[0], 128, False)
+    natural(p1, 0, 128 * frm[1], 128, False)
+    natural(po, CAPP, CAPP * rank, CAPP, True)
+    k_zu2, k_zv = natural(pm, CAPP, CAPP * mate, CAPP, True)
+
     need("cs_", k_pu, k_zu, k_zu2)
     k_g = [done("cs_", s.activation(T.gu[:, 128 * h:128 * h + 128], T.zu[:].indirect(T.pu[:, 16 + 8 * h:24 + 8 * h]), F.Copy)) for h in (0, 1)]
     need("cv", k_zv)

@@ -9,11 +9,12 @@ ST = 528
 NB, USED = ST // B, 86
 LV = 6
 XC = 43 * B
+CUT = {"a": (0, XC), "b": (XC, T_COLS), "": (0, T_COLS)}
 J = 2 * ST
 S0, H0, P0, RG = 0, J, 2 * J, 4 * J
 K = J + 2 * B - 1
 E0 = H0 + 2 * K - B - 1
-BIG = 1e29
+BIG, FAR = 1e29, 1e6
 PHI, LESS = float(2 ** 23 + 1), 1.0 - 2.0 ** -24
 
 
@@ -22,7 +23,19 @@ def shift(m):
 
 
 CH = {"a": (0, 128), "b": (128, 128), "m": (256, 64), "o": (320, 64)}
-WORK = {("a", 0): 2, ("a", 1): 2, ("b", 0): 3, ("b", 1): 3, ("m", 0): 3, ("m", 1): 3, ("o", 0): 3, ("o", 1): 3}
+WORK = {"a0": 1, "a1": 3, "b0": 3, "b1": 3, "m0": 3, "m1": 3, "o0": 3, "o1": 3}
+
+ORDER = {
+    "cv": """one c0 pad0 r1 lm l6 pad1 r6 r r2 c1 sb qa0 nb b6 yy q qxa dd q2 qxb w fd qa1 ac ad ab qa2 of P0a qa3 f0 f1 od
+             S0 n0 P0b P1a P1b S1 L01 h3b P2 L02 P3 L03 S3 L11 L04 S2 L05 L12 Ba00 L06 L13 Ba01 L14 Ca00 L15 n1 Ca01 L16
+             sb00 sb01 Da00 Db00 Db01 Da01 sa10 sa11 Da10 Da11 sb10 sb11 qca Db10 Db11 sm0 sm1 qcb Dm00 Dm01 Dm10 Dm11 so0 qcm
+             so1 Do00 qu Do01 Do10 Do11 qv qco va pu vp vb y0 y1""",
+    "cs_": """ez1 e ne ez3 tc td pad2 pad3 ez0 ez2 zu zv tp h0a h0b h1a h1b h2a h2b h3a
+              Bb0 Aa0 Ab0 Bb1 Ba1 Cb0 Ab1 Aa1 Ca1 Bm0 Cb1 Am0 Cm0 Am1 Bm1 Cm1 Ao0 Bo0 Co0 Ao1 Bo1 Co1 ua ub up g0 g1""",
+    "ct": "z0a z0b z1a z1b z2a z2b z3a z3b Ua Ub Va Up Vp Vb",
+    "cg": "m6 m3",
+}
+LOADS = "x:a a:0 x:b a:1 a:2 a:3"
 
 SCRATCH = {
     "xb": ("sbuf", [128, 2048], "bfloat16"), "ab": ("sbuf", [128, 2048], "bfloat16"),
@@ -32,29 +45,28 @@ SCRATCH = {
     "uq": ("sbuf", [128, 128], "float8_e4m3fn_x4"), "us": ("sbuf", [128, 128], "uint8"),
     "vq": ("sbuf", [128, 128], "float8_e4m3fn_x4"), "vs": ("sbuf", [128, 128], "uint8"),
     "cq": ("sbuf", [128, 384], "float8_e4m3fn_x4"), "cs": ("sbuf", [128, 384], "uint8"),
-    "oq": ("sbuf", [128, 128], "float8_e4m3fn_x4"), "ow": ("sbuf", [128, 128], "uint8"),
-    "rq": ("sbuf", [128, 320], "float8_e4m3fn_x4"), "rs": ("sbuf", [128, 512], "uint8"),
+    "rq": ("sbuf", [128, 256], "float8_e4m3fn_x4"), "rs": ("sbuf", [128, 256], "uint8"),
+    "mq": ("sbuf", [128, 192], "float8_e4m3fn_x4"), "ms": ("sbuf", [128, 384], "uint8"),
     "win": ("sbuf", [128, 2 * RG], "bfloat16"),
-    "tile": ("sbuf", [128, 4 * SL], "bfloat16"),
+    "tile": ("sbuf", [128, 4 * (SL + CAPP)], "bfloat16"),
     "ones": ("sbuf", [128, ST], "bfloat16"), "m6": ("sbuf", [128, ST], "bfloat16"),
-    "m3": ("sbuf", [128, 384], "bfloat16"), "m2": ("sbuf", [128, 512], "bfloat16"),
+    "m2": ("sbuf", [128, 512], "bfloat16"), "m3": ("sbuf", [128, 384], "bfloat16"), "m4": ("sbuf", [128, 512], "bfloat16"),
     "ll": ("sbuf", [128, 4 * NS], "int32"), "qq": ("sbuf", [128, 6 * NS], "float32"),
-    "l6": ("sbuf", [128, 2 * NS], "int32"), "sb": ("sbuf", [128, 2 * NS], "int32"), "b6": ("sbuf", [128, 2 * NS], "float32"),
-    "ee": ("sbuf", [128, 2 * NS], "float32"), "aa": ("sbuf", [128, 2 * NS], "float32"), "tt": ("sbuf", [128, 2 * NS], "float32"),
-    "yy": ("sbuf", [128, 2 * NS], "float32"), "zz": ("sbuf", [128, 2 * NS], "float32"), "z2": ("sbuf", [128, 2 * NS], "float32"),
-    "dd": ("sbuf", [128, 2 * NS], "float32"), "fd": ("sbuf", [128, 2 * NS], "float32"),
-    "of": ("sbuf", [128, 4, NS], "float32"),
-    "o1": ("sbuf", [128, 9, 16], "uint16"), "o2": ("sbuf", [128, 6, 8], "uint16"), "od": ("sbuf", [128, NS], "uint16"),
-    "pl": ("sbuf", [128, 32], "int32"), "pz": ("sbuf", [128, 16], "int32"), "pu": ("sbuf", [128, 32], "uint16"),
-    "zu": ("sbuf", [128, 400], "float32"), "zv": ("sbuf", [128, 384], "float32"),
+    "l6": ("sbuf", [128, 2 * NS], "int32"), "sb": ("sbuf", [128, 2 * NS], "int32"), "ee": ("sbuf", [128, 2 * NS], "float32"),
+    "dd": ("sbuf", [128, 2 * NS], "float32"), "sg": ("sbuf", [128, 2 * NS], "float32"), "fd": ("sbuf", [128, 2 * NS], "float32"),
+    "d0": ("sbuf", [128, 6 * NS], "float32"), "d1": ("sbuf", [128, 6 * NS], "float32"),
+    "of": ("sbuf", [128, 12 * NS], "float32"),
+    "o1": ("sbuf", [128, 9, 32], "uint16"), "o2": ("sbuf", [128, 6, 16], "uint16"), "od": ("sbuf", [128, NS], "uint16"),
+    "pl": ("sbuf", [128, 32], "int32"), "pu": ("sbuf", [128, 32], "uint16"),
+    "zu": ("sbuf", [128, SL + 1], "float32"), "zv": ("sbuf", [128, SL + 1], "float32"),
     "gu": ("sbuf", [128, P], "float32"), "yb": ("sbuf", [128, P], "float32"),
     "zp": ("psum", [128, 2048], "float32"), "pp": ("psum", [128, 2048], "float32"),
 }
-for (_h, _p), _w in WORK.items():
-    SCRATCH["g%s%d" % (_h, _p)] = ("sbuf", [128, 2 * _w * CH[_h][1]], "bfloat16")
-    SCRATCH["s%s%d" % (_h, _p)] = ("sbuf", [128, 2 * _w * CH[_h][1]], "bfloat16")
-    SCRATCH["c%s%d" % (_h, _p)] = ("sbuf", [128, 2 * CH[_h][1]], "bfloat16")
-SEMAPHORES = ["cv", "cs_", "ct", "cg", "lists", "x0", "x1", "a0", "a1", "a2", "a3", "uv", "pfg", "y0", "y1", "arr0", "arr1", "arr2", "sent"]
+for _u, _w in WORK.items():
+    SCRATCH["g" + _u[0]] = ("sbuf", [128, 2 * (WORK[_u[0] + "0"] + WORK[_u[0] + "1"]) * CH[_u[0]][1]], "bfloat16")
+    SCRATCH["s" + _u] = ("sbuf", [128, 2 * _w * CH[_u[0]][1]], "bfloat16")
+    SCRATCH["c" + _u] = ("sbuf", [128, 2 * CH[_u[0]][1]], "bfloat16")
+SEMAPHORES = ["cv", "cs_", "ct", "cg", "lists", "uv", "pfg", "y0", "y1", "arr0", "arr1", "arr2", "sent"] + LOADS.replace(":", "").split()
 
 
 def rank_program(g, core, T, topo):
@@ -63,31 +75,52 @@ def rank_program(g, core, T, topo):
         return
     A, F = AluOpType, ActivationFunctionType
     que = {"cv": g.vector, "cs_": g.scalar, "ct": g.tensor, "cg": g, "sy": g.sync}
-    count = {k: 0 for k in que}
-    seen = {k: {} for k in que}
+    order = {q: names.split() for q, names in ORDER.items()}
     v, s, t = g.vector, g.scalar, g.tensor
-    pair, mate = rank // 2, rank ^ 1
+    ts, tt, scan = v.tensor_scalar, v.tensor_tensor, v.tensor_tensor_scan
+    pair, mate, odd = rank // 2, rank ^ 1, rank % 2
     to = {"a": (pair + 1) % 3, "b": (pair + 2) % 3}
-    frm = [(pair + 2) % 3, (pair + 1) % 3]
+    frm = {"a": (pair + 2) % 3, "b": (pair + 1) % 3}
+    eng = topo.engines(core, T.cores[mate])
 
-    def need(q, *toks):
-        for sem, val in toks:
-            if seen[q].get(sem, 0) < val:
-                que[q].wait_ge(T.sem[sem], val)
-                seen[q][sem] = val
+    when = {name: [(q, k + 1)] for q in order for k, name in enumerate(order[q])}
+    when.update({"in": [("lists", 32)], "uv": [("uv", 32)], "pfg": [("pfg", 256)]})
+    when.update({"in" + x.replace(":", ""): [(x.replace(":", ""), 16)] for x in LOADS.split()})
+    when.update({"arr" + h: [("arr%d" % k, n * len(eng))] for k, (h, n) in enumerate((("a", 2), ("b", 2), ("m", 1)))})
+    seen = {q: {} for q in que}
+    calls = {}
 
-    def done(q, ins):
-        ins.then_inc(T.sem[q], 1)
-        count[q] += 1
-        return (q, count[q])
+    def need(q, names):
+        for name in names.split():
+            for sem, val in when[name]:
+                if seen[q].get(sem, 0) < val:
+                    que[q].wait_ge(T.sem[sem], val)
+                    seen[q][sem] = val
+
+    def call(name, reads, fn, *args, **kw):
+        calls[name] = (reads, fn, args, kw)
+
+    def alias(name, *parts):
+        if name not in when and all(x in when for x in parts):
+            when[name] = [x for part in parts for x in when[part]]
+
+    def copy(name, reads, out, src):
+        if name in order["cv"]:
+            call(name, reads, v.tensor_copy, out, src)
+        else:
+            call(name, reads, s.activation, out, src, F.Copy)
+
+    def zero(name, out, n):
+        if name in order["cv"]:
+            call(name, "", v.memset, out, 0.0)
+        else:
+            call(name, "one", s.activation, out, T.ones[:, 0:n], F.Copy, scale=0.0)
 
     s.dma_start(T.ll[:, 0:NS], T.ln[:]).then_inc(T.sem.lists, 16)
     g.sync.dma_start(T.ll[:, 2 * NS:3 * NS], T.lo[:]).then_inc(T.sem.lists, 16)
-    g.sync.dma_start(T.xb[:, 0:4 * XC], T.x[:, 0:4 * XC]).then_inc(T.sem.x0, 16)
-    s.dma_start(T.ab[:, 0:512], T.a[:, 0:512]).then_inc(T.sem.a0, 16)
-    g.sync.dma_start(T.xb[:, 4 * XC:2048], T.x[:, 4 * XC:2048]).then_inc(T.sem.x1, 16)
-    for i in (1, 2, 3):
-        g.sync.dma_start(T.ab[:, 512 * i:512 * i + 512], T.a[:, 512 * i:512 * i + 512]).then_inc(T.sem["a%d" % i], 16)
+    for k, (x, c) in enumerate(w.split(":") for w in LOADS.split()):
+        a, b = (4 * CUT[c][0], 4 * CUT[c][1]) if x == "x" else (512 * int(c), 512 * int(c) + 512)
+        (s if k == 1 else g.sync).dma_start(T[x + "b"][:, a:b], T[x][:, a:b]).then_inc(T.sem[x + c], 16)
     g.sync.dma_start(T.ub[:], T.u[:]).then_inc(T.sem.uv, 16)
     g.sync.dma_start(T.vb[:], T.v[:]).then_inc(T.sem.uv, 16)
     for k in range(8):
@@ -97,287 +130,214 @@ def rank_program(g, core, T, topo):
     def at(i):
         return (i // 2) * RG + (i % 2) * ST
 
-    k_one = done("cv", v.memset(T.ones[:], 1.0))
+    call("one", "", v.memset, T.ones[:], 1.0)
+    call("c0", "", v.memset, T.d0[:, 0::3], FAR)
+    call("c1", "", v.memset, T.d1[:, 2::3], FAR)
     for i in range(4):
-        k_hp = done("cv", v.memset(T.win[:, at(i) + H0 + T_COLS:at(i) + H0 + ST], 0.0))
-    k_zu = done("cv", v.memset(T.zu[:, 384:400], 0.0))
-
-    need("cg", k_one)
-
-    def mask(out, n, b):
-        return done("cg", g.affine_select(out, T.ones[:, 0:n], [[0, n // b], [1, b]], A.is_gt, 0.0, 0, 0))
-
-    k_m6 = mask(T.m6[:], ST, B)
-    k_ms = {2: mask(T.m2[:], 512, 2), 3: mask(T.m3[:], 384, 3)}
-
-    need("cs_", k_one)
+        zero("pad%d" % i, T.win[:, at(i) + H0 + T_COLS:at(i) + H0 + ST], ST - T_COLS)
+    zero("zu", T.zu[:, 0:1], 1)
+    zero("zv", T.zv[:, 0:1], 1)
+    zero("tp", T.tile[:, 4 * SL:4 * (SL + CAPP)], 4 * CAPP)
+    for b, n in ((B, ST), (2, 512), (3, 384), (4, 512)):
+        call("m%d" % b, "one", g.affine_select, T["m%d" % b][:], T.ones[:, 0:n], [[0, n // b], [1, b]], A.is_gt, 0.0, 0, 0)
     lead, tail = E0 + shift(LV), E0 + shift(LV) + B * (NB + USED - 2 ** LV) + 1
     for p in range(2):
-        for a, b in ((P0 + J, lead), (tail, RG)):
-            k_ez = done("cs_", s.activation(T.win[:, p * RG + a:p * RG + b], T.ones[:, 0:b - a], F.Copy, scale=0.0))
+        for k, (a, b) in enumerate(((P0 + J, lead), (tail, RG))):
+            zero("ez%d" % (2 * p + k), T.win[:, p * RG + a:p * RG + b], b - a)
 
-    def vec(call, *args, deps=()):
-        need("cv", *deps)
-        return done("cv", call(*args))
-
-    def act(out, src, f, scale, *deps):
-        need("cs_", *deps)
-        return done("cs_", s.activation(out, src, f, scale=scale))
-
-    ts, tt = v.tensor_scalar, v.tensor_tensor
     lo_, hi_ = slice(0, NS), slice(NS, 2 * NS)
     n_, L_, R_, LR, RL = T.ll[:, lo_], T.ll[:, 2 * NS:3 * NS], T.ll[:, 3 * NS:4 * NS], T.ll[:, 2 * NS:4 * NS], T.ll[:, NS:3 * NS]
     lm_, r1_, nb_, q_, q2_, w_ = (T.qq[:, k * NS:(k + 1) * NS] for k in range(6))
-    todo = [
-        ("r1", "in", tt, r1_, L_, n_, A.add),
-        ("lm", "in", ts, lm_, n_, -1, None, A.add),
-        ("l6", "in", ts, T.l6[:, lo_], L_, B, 683, A.add, A.mult),
-        ("e", "in", ts, T.ee[:, lo_], n_, -1, 1, A.add, A.min),
-        ("r6", "r1", ts, T.l6[:, hi_], r1_, -1, 683, A.add, A.mult),
-        ("r", "lm", tt, R_, L_, lm_, A.add),
-        ("r2", "r1", ts, T.ll[:, hi_], r1_, 1, None, A.add),
-        ("ne", "lm", ts, T.ee[:, hi_], lm_, -1, -1, A.mult, A.max),
-        ("sb", "r6", ts, T.sb[:], T.l6[:], 12, None, A.arith_shift_right),
-        ("yy", "ne", tt, T.yy[:], LR, T.ee[:], A.add),
-        ("nb", "sb", tt, nb_, T.sb[:, hi_], T.sb[:, lo_], A.subtract),
-        ("b6", "sb", ts, T.b6[:], T.sb[:], B, -B - 0.25, A.mult, A.add),
-        ("q", "nb", ts, q_, nb_, PHI, None, A.mult),
-        ("q2", "nb", ts, q2_, nb_, PHI, LESS, A.mult, A.mult),
-        ("tc", "nb", ts, T.tt[:, lo_], nb_, 2, K, A.min, A.mult),
-        ("td", "nb", ts, T.tt[:, hi_], nb_, 2, K, A.min, A.mult),
-        ("dd", "b6", tt, T.dd[:], T.b6[:], RL, A.subtract),
-        ("w", "q2", tt, w_, q_, q2_, A.subtract),
-        ("zz", "td", tt, T.zz[:], T.b6[:], T.tt[:], A.add),
-        ("fd", "dd", ts, T.fd[:], T.dd[:], -B - 0.5, J, A.is_ge, A.mult),
-        ("ac", "w", ts, T.aa[:, lo_], w_, 0, 1 / 3, A.max, A.mult),
-        ("ad", "w", ts, T.aa[:, hi_], w_, 0, 1 / 3 - B, A.max, A.mult),
-        ("z2", "zz", tt, T.z2[:], T.zz[:], T.yy[:], A.max),
-        ("ab", "fd", tt, T.of[:, 0:2, :], LR, T.fd[:], A.add),
-        ("of", "z2", tt, T.of[:, 2:4, :], T.z2[:], T.aa[:], A.add),
-        ("o0", "of", ts, T.o1[:, :, 0:8], T.of[:, 0:3, :], 0, None, A.add),
-        ("o1", "of", ts, T.o1[:, :, 8:16], T.of[:, 0:3, :], ST, None, A.add),
-        ("od", "of", v.tensor_copy, T.od[:], T.of[:, 3, :]),
-        ("o2", "of", ts, T.o2[:, :, 0:4], T.of[:, 0:3, 8 * pair:8 * pair + 8], 0, None, A.add),
-        ("o3", "of", ts, T.o2[:, :, 4:8], T.of[:, 0:3, 8 * pair:8 * pair + 8], ST, None, A.add),
-    ]
-    made = {"in": ("lists", 32)}
-
-    def lists(upto):
-        while upto not in made:
-            name, reads, *call = todo[len(made) - 1]
-            made[name] = vec(*call, deps=[made[reads]])
-
-    def quant(out, sc, src, *deps):
-        need("cv", *deps)
-        return done("cv", v.quantize_mx(out, sc, src))
-
-    def quant_a(i):
-        return quant(T.aq[:, 128 * i:128 * i + 128], T.sa[:, 128 * i:128 * i + 128], T.ab[:, 512 * i:512 * i + 512], ("a%d" % i, 16))
-
-    def mm(out, w, ws, x, xs, *deps):
-        need("ct", *deps)
-        return done("ct", t.matmul_mx(out, w, ws, x, xs, True, True))
-
-    k_h = {}
+    b6_, yy_ = T.d1[:, 0::3], T.d1[:, 1::3]
+    tc_, td_, ac_, ad_ = T.d0[:, 1:3 * NS:3], T.d0[:, 3 * NS + 1::3], T.d0[:, 2:3 * NS:3], T.d0[:, 3 * NS + 2::3]
+    base = -B - 0.25 + (0 if "tc" in order["cv"] else 2 * K)
+    call("r1", "in", tt, r1_, L_, n_, A.add)
+    call("lm", "in", ts, lm_, n_, -1, None, A.add)
+    call("l6", "in", ts, T.l6[:, lo_], L_, B, 683, A.add, A.mult)
+    call("r6", "r1", ts, T.l6[:, hi_], r1_, -1, 683, A.add, A.mult)
+    call("r", "lm", tt, R_, L_, lm_, A.add)
+    call("r2", "r1", ts, T.ll[:, hi_], r1_, 1, None, A.add)
+    call("e", "lm", s.activation, T.ee[:, hi_], lm_, F.Sign)
+    call("ne", "lm", s.activation, T.ee[:, lo_], lm_, F.Sign, scale=-1.0)
+    call("sb", "l6 r6", ts, T.sb[:], T.l6[:], 12, None, A.arith_shift_right)
+    call("yy", "r e ne", tt, yy_, T.ee[:], LR, A.subtract)
+    call("nb", "sb", tt, nb_, T.sb[:, hi_], T.sb[:, lo_], A.subtract)
+    call("b6", "sb", ts, b6_, T.sb[:], -B, base, A.mult, A.subtract)
+    if "q" in order["cv"]:
+        call("q", "nb", ts, q_, nb_, 0, PHI, A.max, A.mult)
+    else:
+        call("q", "nb", s.activation, q_, nb_, F.Relu, scale=PHI)
+    if "q2" in order["cv"]:
+        call("q2", "q", ts, q2_, q_, LESS, None, A.mult)
+    else:
+        call("q2", "q", s.activation, q2_, q_, F.Copy, scale=LESS)
+    call("w", "q q2", tt, w_, q_, q2_, A.subtract)
+    call("dd", "b6 r2", tt, T.dd[:], b6_, RL, A.add)
+    call("sg", "dd", s.activation, T.sg[:], T.dd[:], F.Sign, bias=base - 0.25)
+    if "sg" in when:
+        call("fd", "sg", s.activation, T.fd[:], T.sg[:], F.Identity, bias=-J / 2, scale=J / 2)
+    else:
+        call("fd", "dd", ts, T.fd[:], T.dd[:], 0.25 - base, -J, A.is_le, A.mult)
+    call("ab", "fd r", tt, T.of[:, 2:6 * NS:3], T.fd[:], LR, A.subtract)
+    for name, out in (("tc", tc_), ("td", td_)):
+        if name in order["cv"]:
+            call(name, "nb", ts, out, nb_, 2, -K, A.min, A.mult)
+        else:
+            call(name, "nb", s.activation, out, nb_, F.Relu, bias=2.0 * K, scale=-1.0 * K)
+    for name, out, c in (("ac", ac_, -1 / 3), ("ad", ad_, B - 1 / 3)):
+        if name in order["cv"]:
+            call(name, "w", ts, out, w_, c, None, A.mult)
+        else:
+            call(name, "w", s.activation, out, w_, F.Copy, scale=c)
+    if "e" in order["cv"]:
+        call("e", "in", ts, T.ee[:, hi_], n_, -1, 1, A.add, A.min)
+        call("ne", "lm", ts, T.ee[:, lo_], lm_, -1, -1, A.mult, A.max)
+    call("of", "c0 c1 b6 yy tc td ac ad", scan, T.of[:, 6 * NS:12 * NS], T.d0[:], T.d1[:], 0.0, A.add, A.min)
+    for i in range(4):
+        call("f%d" % i, "ab of", ts, T.o1[:, :, 8 * i:8 * i + 8], T.of[:, 2:9 * NS:3], -1, at(i), A.mult, A.add)
+        call("n%d" % i, "f%d" % i, v.tensor_copy, T.o2[:, :, 4 * i:4 * i + 4], T.o1[:, pair::3, 8 * i:8 * i + 8])
+    call("od", "of", ts, T.od[:], T.of[:, 9 * NS + 2::3], -1, None, A.mult)
 
     def bank(k, a, b):
         return T.zp[:, 512 * k + a:512 * k + b] if k < 4 else T.pp[:, 512 * (k - 4) + a:512 * (k - 4) + b]
 
-    def product(i, a, b, ps, *deps):
-        k = mm(bank(ps, 0, b - a), T.aq[:, 128 * i:128 * i + 128], T.sa[:, 128 * i:128 * i + 128], T.xq[:, a:b], T.xs[:, a:b], *deps)
-        k_h[i, a] = act(T.win[:, at(i) + H0 + a:at(i) + H0 + b], bank(ps, 0, b - a), F.Relu, 0.05, k)
+    def cover(name):
+        own = [c for c in CUT if name + c in when]
+        for c, (a, b) in CUT.items():
+            alias(name + c, *[name + d for d in own if CUT[d][0] < b and a < CUT[d][1]])
 
-    scan = v.tensor_tensor_scan
+    cover("qx")
+    for c in "ab":
+        a, b = CUT[c]
+        call("qx" + c, "inx" + c, v.quantize_mx, T.xq[:, a:b], T.xs[:, a:b], T.xb[:, 4 * a:4 * b])
+    products = [name for name in order["ct"] if name[0] == "z"]
+    for i in range(4):
+        w, aq, sa = at(i) + H0, T.aq[:, 128 * i:128 * i + 128], T.sa[:, 128 * i:128 * i + 128]
+        call("qa%d" % i, "ina%d" % i, v.quantize_mx, aq, sa, T.ab[:, 512 * i:512 * i + 512])
+        for x in "hPS":
+            cover(x + str(i))
+        for c, (a, b) in CUT.items():
+            z = "z%d%s" % (i, c)
+            if z in products:
+                ps = bank(products.index(z), 0, b - a)
+                call(z, "qa%d qx%s" % (i, c), t.matmul_mx, ps, aq, sa, T.xq[:, a:b], T.xs[:, a:b], True, True)
+                if "h" + z[1:] in order["cv"]:
+                    call("h" + z[1:], z, ts, T.win[:, w + a:w + b], ps, 0.0, 0.05, A.max, A.mult)
+                else:
+                    call("h" + z[1:], z, s.activation, T.win[:, w + a:w + b], ps, F.Relu, scale=0.05)
+            b, reads = b if b < T_COLS else ST, "m6 pad%d h%d%s" % (i, i, c)
+            call("P%d%s" % (i, c), reads, scan, T.win[:, w + J + a:w + J + b], T.m6[:, a:b], T.win[:, w + a:w + b], 0.0, A.mult, A.max)
+            end = w - J + a - 1 if w - J + a else None
+            call("S%d%s" % (i, c), reads, scan, T.win[:, w - J + b - 1:end:-1], T.m6[:, 0:b - a], T.win[:, w + b - 1:w + a - 1:-1], 0.0, A.mult, A.max)
+    for p in range(2):
+        alias("L%d0" % p, "P%d" % (2 * p), "P%d" % (2 * p + 1), "ez%d" % (2 * p), "ez%d" % (2 * p + 1))
+        for m in range(1, LV + 1):
+            n = B * (NB + USED - 2 ** m) + 1
+            a = p * RG + (E0 + shift(m - 1) if m > 1 else P0 + B - 1)
+            b, o = a + B * 2 ** (m - 1), p * RG + E0 + shift(m)
+            call("L%d%d" % (p, m), "L%d%d" % (p, m - 1), scan, T.win[:, o:o + n:B], T.win[:, a:a + n:B], T.win[:, b:b + n:B], BIG, A.min, A.max)
 
-    def prefix(i, a, b, *deps):
-        w = at(i)
-        return vec(scan, T.win[:, w + P0 + a:w + P0 + b], T.m6[:, a:b], T.win[:, w + H0 + a:w + H0 + b], 0.0, A.mult, A.max, deps=(k_m6, k_hp) + deps)
+    WIN = [(S0, P0), (H0, P0 + J), (H0, RG), (H0, RG)]
+    for u, w in WORK.items():
+        h, p = u[0], int(u[1])
+        (c, n), who = CH[h], {"m": mate, "o": rank}.get(h)
+        kind = "f" if h in to else "n"
+        lists = "%s0 %s1" % (kind, kind)
+        tables = ["S%d S%d" % (2 * p, 2 * p + 1), "P%d P%d" % (2 * p, 2 * p + 1), "L%d%d" % (p, LV), "L%d%d" % (p, LV)]
+        gat, top, third = T["g" + h], T["s" + u], T["c" + u]
+        g0 = 2 * p * WORK[h + "0"] * n
 
-    def suffix(i, *deps):
-        w = at(i)
-        end = w + S0 - 1 if w + S0 else None
-        return vec(scan, T.win[:, w + S0 + ST - 1:end:-1], T.m6[:], T.win[:, w + H0 + ST - 1:w + H0 - 1:-1], 0.0, A.mult, A.max, deps=(k_m6, k_hp) + deps)
+        def part(e, j0, j1):
+            a, b = WIN[e]
+            off = T.o1[:, 3 * e + to[h], 8 * j0:8 * j1] if h in to else T.o2[:, 2 * e + who % 2, 4 * j0:4 * j1]
+            if j1 > 2:
+                return T.win[:, a:RG + b].indirect(off)
+            return T.win[:, p * RG + a:p * RG + b].indirect(off)
 
-    k_e = {}
+        for e in range(w):
+            x = "ABCE"[e]
+            call(x + u, lists + " " + tables[e], s.activation, gat[:, g0 + e:g0 + 2 * w * n:w], part(e, 0, 2), F.Copy)
+            if p and x + h in when:
+                call(x + h, "%s %s2 %s3 S0 S1 L0%d %s" % (lists, kind, kind, LV, tables[e]), s.activation, gat[:, e:4 * w * n:w], part(e, 0, 4), F.Copy)
+            alias(x + u, x + h)
+        got = "m%d " % w + " ".join("ABCE"[e] + u for e in range(w))
+        before = ["", "A", "s" if w == 2 else "B", "s" if w == 3 else "C"]
 
-    def level(p, m, *deps):
-        n = NB + USED + 1 - 2 ** m
-        a = p * RG + (E0 + shift(m - 1) if m > 1 else P0 + B - 1)
-        b, o = a + B * 2 ** (m - 1), p * RG + E0 + shift(m)
-        k_e[p] = vec(scan, T.win[:, o:o + B * (n - 1) + 1:B], T.win[:, a:a + B * (n - 1) + 1:B], T.win[:, b:b + B * (n - 1) + 1:B],
-                     BIG, A.min, A.max, deps=(k_ez, k_e[p]))
+        def held(e, a, b):
+            if e == w:
+                return top[:, w * a + w - 1:w * b:w] if w > 1 else gat[:, g0 + a:g0 + b]
+            return (top if e == 2 else third)[:, a:b]
 
-    WIN = [(S0, P0), (H0, P0 + J), (H0, RG)]
+        for x in "sABC":
+            alias(x + u, x + u + "0", x + u + "1")
+            alias(x + u + "0", x + u)
+            alias(x + u + "1", x + u)
+        for x, (j0, j1) in {"": (0, 2), "0": (0, 1), "1": (1, 2)}.items():
+            a, b = n * j0, n * j1
+            if w > 1 and w * (b - a) <= SCRATCH["m%d" % w][1][1]:
+                call("s" + u + x, got, scan, top[:, w * a:w * b], T["m%d" % w][:, 0:w * (b - a)], gat[:, g0 + w * a:g0 + w * b], 0.0, A.mult, A.max)
+            for e in range(w, 3):
+                call("ABC"[e] + u + x, "%s %s %s" % (lists, tables[e], before[e] + u + x), tt, held(e + 1, a, b), part(e, j0, j1), held(e, a, b), A.max)
+        for j in range(2):
+            name, out = "D%s%d" % (u, j), T.tile[:, 4 * c + 2 * p + j:4 * (c + n):4]
+            if w < 4:
+                o = 8 * to[h] if h in to else 4 * who
+                src = T.win[:, at(2 * p + j) + H0:p * RG + RG].indirect(T.od[:, o:o + n // 16])
+                call(name, "od %s%s%d" % (before[3], u, j), tt, out, src, held(3, n * j, n * j + n), A.max)
+            else:
+                copy(name, "s%s%d" % (u, j), out, held(4, n * j, n * j + n))
+    for h in CH:
+        alias("D" + h, *["D%s%d%d" % (h, p, j) for p in range(2) for j in range(2)])
+    place = {"a": 128 * odd, "b": 128 + 128 * odd, "m": 256 - 256 * odd}
+    for h, (c, reads) in {"a": (0, "Da"), "b": (128, "Db"), "m": (192, "Db Dm")}.items():
+        o = place[h]
+        call("qc" + h, reads, v.quantize_mx, T.cq[:, o:o + 128], T.cs[:, o:o + 128], T.tile[:, 4 * c:4 * c + 512])
+    c, oq, os_ = (320, CAPP, 256) if odd else (256, 0, 0)
+    call("qco", "Dm Do tp", v.quantize_mx, T.mq[:, oq:oq + 128], T.ms[:, os_:os_ + 128], T.tile[:, 4 * c:4 * c + 512])
 
-    def part(h, p, e, js=(0, 2)):
-        a, b = WIN[e]
-        if h in to:
-            off = T.o1[:, 3 * e + to[h], 8 * js[0]:8 * js[1]]
-        else:
-            off = T.o2[:, 2 * e + (mate if h == "m" else rank) % 2, 4 * js[0]:4 * js[1]]
-        return T.win[:, p * RG + a:p * RG + b].indirect(off)
-
-    got, k_s, k_t = {}, {}, {}
-
-    def gather(h, p, es, *deps):
-        w, n = WORK[h, p], 2 * CH[h][1]
-        for e in es:
-            if e < w:
-                need("cs_", *deps)
-                got[h, p] = done("cs_", s.activation(T["g%s%d" % (h, p)][:, e:w * n:w], part(h, p, e), F.Copy))
-
-    def best(h, p, *js):
-        w = WORK[h, p]
-        a, b = w * CH[h][1] * js[0], w * CH[h][1] * (js[-1] + 1)
-        k = vec(scan, T["s%s%d" % (h, p)][:, a:b], T["m%d" % w][:, 0:b - a], T["g%s%d" % (h, p)][:, a:b], 0.0, A.mult, A.max, deps=[k_ms[w], got[h, p]])
-        for j in js:
-            k_s[h, p, j] = k
-
-    def third(h, p, *js):
-        a, b = CH[h][1] * js[0], CH[h][1] * (js[-1] + 1)
-        k = vec(tt, T["c%s%d" % (h, p)][:, a:b], part(h, p, 2, (js[0], js[-1] + 1)), T["s%s%d" % (h, p)][:, 2 * a + 1:2 * b:2], A.max,
-                deps=[k_e[p], k_s[h, p, js[-1]]])
-        for j in js:
-            k_s[h, p, j] = k
-
-    def last(h, p, j):
-        w, (c, n) = WORK[h, p], CH[h]
-        o = 8 * to[h] if h in to else 4 * (mate if h == "m" else rank)
-        cur = T["s%s%d" % (h, p)][:, 3 * n * j + 2:3 * n * (j + 1):3] if w == 3 else T["c%s%d" % (h, p)][:, n * j:n * (j + 1)]
-        src = T.win[:, at(2 * p + j) + H0:p * RG + RG].indirect(T.od[:, o:o + n // 16])
-        k_t[h] = vec(tt, T.tile[:, 4 * c + 2 * p + j:4 * (c + n):4], src, cur, A.max, deps=[made["od"], k_s[h, p, j]])
-
-    k_c = {}
-
-    def pack(h):
-        c, o = {"a": (0, 128), "b": (128, 256), "m": (192, 0)}[h]
-        k_c[h] = quant(T.cq[:, o:o + 128], T.cs[:, o:o + 128], T.tile[:, 4 * c:4 * c + 512], k_t[h])
-
-    lists("b6")
-    k_x0 = quant(T.xq[:, 0:XC], T.xs[:, 0:XC], T.xb[:, 0:4 * XC], ("x0", 16))
-    product(0, 0, XC, 0, k_x0, quant_a(0))
-    lists("dd")
-    k_x1 = quant(T.xq[:, XC:512], T.xs[:, XC:512], T.xb[:, 4 * XC:2048], ("x1", 16))
-    product(0, XC, 512, 7, k_x1)
-    lists("fd")
-    product(1, 0, XC, 1, quant_a(1))
-    product(1, XC, 512, 6)
-    prefix(0, 0, XC, k_h[0, 0])
-    lists("ab")
-    product(2, 0, 512, 2, quant_a(2))
-    lists("of")
-    suffix(0, k_h[0, XC])
-    product(3, 0, 512, 3, quant_a(3))
-    prefix(0, XC, ST)
-    lists("o1")
-    k_e[0] = prefix(1, 0, ST, k_h[1, XC])
-    gather("a", 0, (0, 1), made["o1"], suffix(1))
-    level(0, 1)
-    suffix(2, k_h[2, 0])
-    level(0, 2)
-    prefix(2, 0, ST)
-    level(0, 3)
-    k_e[1] = prefix(3, 0, ST, k_h[3, 0])
-    level(0, 4)
-    gather("a", 1, (0, 1), suffix(3))
-    level(0, 5)
-    level(1, 1)
-    lists("o3")
-    level(0, 6)
-    gather("b", 0, (0, 1, 2), k_e[0])
-    level(1, 2)
-    best("a", 0, 0, 1)
-    level(1, 3)
-    third("a", 0, 0)
-    level(1, 4)
-    third("a", 0, 1)
-    level(1, 5)
-    last("a", 0, 0)
-    level(1, 6)
-    gather("b", 1, (0, 1, 2), k_e[1])
-    for h in "mo":
-        for p in range(2):
-            gather(h, p, (0, 1, 2), made["o3"])
-    best("a", 1, 0, 1)
-    last("a", 0, 1)
-    k_u = quant(T.uq[:], T.us[:], T.ub[:], ("uv", 32))
-    k_v = quant(T.vq[:], T.vs[:], T.vb[:], ("uv", 32))
-    third("a", 1, 0)
-    third("a", 1, 1)
-    last("a", 1, 0)
-    last("a", 1, 1)
-    best("b", 0, 0)
-    best("b", 0, 1)
-    pack("a")
-    last("b", 0, 0)
-    last("b", 0, 1)
-    best("b", 1, 0)
-    best("b", 1, 1)
-    last("b", 1, 0)
-    last("b", 1, 1)
-    best("m", 0, 0, 1)
-    pack("b")
-    last("m", 0, 0)
-    best("m", 1, 0, 1)
-    last("m", 0, 1)
-    last("m", 1, 0)
-    last("m", 1, 1)
-    best("o", 0, 0, 1)
-    pack("m")
-
-    def transfer(r, es, src, out, h):
-        rid, pnc = topo.addr(T.cores[r])[0:2]
-        return RemoteDMATransfer(dst_ids=[DstId(rid=rid, pnc=pnc)], dma_engine_mask=sum(1 << e for e in es), remote_sem=T.sem["arr%d" % h], src=src, dst=out)
-
-    eng = topo.engines(core, T.cores[mate])
-    half = [eng[0::2], eng[1::2]]
+    call("qu", "uv", v.quantize_mx, T.uq[:], T.us[:], T.ub[:])
+    call("qv", "uv", v.quantize_mx, T.vq[:], T.vs[:], T.vb[:])
+    call("pu", "pfg", ts, T.pu[:], T.pl[:], 1, None, A.add)
+    oq, os_ = (0, 192) if odd else (CAPP, CAPP)
+    second = {"a": (T.rq[:, 0:128], T.rs[:, 0:128], "arra", frm["a"]), "b": (T.rq[:, 128:256], T.rs[:, 128:256], "arrb", frm["b"]),
+              "p": (T.mq[:, oq:oq + 128], T.ms[:, os_:os_ + 128], "qco arrm", pair)}
+    for k, (h, (x, xs, reads, o)) in enumerate(second.items()):
+        for j, (name, w, ws, out) in enumerate((("u", T.uq, T.us, T.zu), ("v", T.vq, T.vs, T.zv))):
+            ps = bank(2 * k + j, 0, 128)
+            call(name.upper() + h, "h0 h1 h2 h3 q%s %s" % (name, reads), t.matmul_mx, ps, w[:], ws[:], x, xs, True, True)
+            copy(name + h, name.upper() + h, out[:, 128 * o + 1:128 * o + 129], ps)
     for h in range(2):
-        need("cg", k_c["ab"[h]])
-        a, b = 128 * h + 128, 128 * h + CAPP * (rank % 2)
-        ds = [(2 * to["ab"[h]] + j, a + CAPP * j) for j in range(2)]
-        g.remote_dma_fused([transfer(r, half[j], T.cq[:, c:c + CAPP].bitcast(dt.uint8), T.rq[:, b:b + CAPP].bitcast(dt.uint8), h)
+        a, b = 128 * h, 128 * h + 128
+        call("g%d" % h, "pu zu ua ub up", s.activation, T.gu[:, a:b], T.zu[:].indirect(T.pu[:, 16 + 8 * h:24 + 8 * h]), F.Copy)
+        call("y%d" % h, "pu zv va vb vp g%d" % h, tt, T.yb[:, a:b], T.zv[:].indirect(T.pu[:, 8 * h:8 * h + 8]), T.gu[:, a:b], A.add)
+
+    for q in order:
+        for name in order[q]:
+            reads, fn, args, kw = calls[name]
+            need(q, reads)
+            fn(*args, **kw).then_inc(T.sem[q], 1)
+
+    def transfer(r, es, src, out, k):
+        rid, pnc = topo.addr(T.cores[r])[0:2]
+        return RemoteDMATransfer(dst_ids=[DstId(rid=rid, pnc=pnc)], dma_engine_mask=sum(1 << e for e in es), remote_sem=T.sem["arr%d" % k], src=src, dst=out)
+
+    half = [eng[0::2], eng[1::2]]
+    for k, h in enumerate("ab"):
+        need("cg", "qc" + h)
+        b = 128 * k + CAPP * odd
+        ds = [(2 * to[h] + j, place[h] + CAPP * j) for j in range(2)]
+        g.remote_dma_fused([transfer(r, half[j], T.cq[:, c:c + CAPP].bitcast(dt.uint8), T.rq[:, b:b + CAPP].bitcast(dt.uint8), k)
                             for j, (r, c) in enumerate(ds)], local_sem=T.sem.sent)
-        g.remote_dma_fused([transfer(r, half[j], T.cs[:, c:c + CAPP], T.rs[:, b:b + CAPP], h) for j, (r, c) in enumerate(ds)], local_sem=T.sem.sent)
-    need("cg", k_c["m"])
-    g.remote_dma_fused([transfer(mate, half[0], T.cq[:, CAPP:128].bitcast(dt.uint8), T.rq[:, 256:320].bitcast(dt.uint8), 2),
-                        transfer(mate, half[1], T.cs[:, CAPP:CAPP + 256], T.rs[:, 256:512], 2)], local_sem=T.sem.sent)
-    sent, arrive = 5 * len(eng), [2 * len(eng), 2 * len(eng), len(eng)]
+        g.remote_dma_fused([transfer(r, half[j], T.cs[:, c:c + CAPP], T.rs[:, b:b + CAPP], k) for j, (r, c) in enumerate(ds)], local_sem=T.sem.sent)
+    need("cg", "qca qcb qcm")
+    c, b, a, o = place["m"] + CAPP, 128 * odd, 128 - CAPP * odd, 128 * odd
+    g.remote_dma_fused([transfer(mate, half[0], T.cq[:, c:c + CAPP].bitcast(dt.uint8), T.mq[:, b:b + CAPP].bitcast(dt.uint8), 2),
+                        transfer(mate, half[1], T.cs[:, a:a + 256], T.ms[:, o:o + 256], 2)], local_sem=T.sem.sent)
+    g.wait_ge(T.sem.sent, 5 * len(eng))
 
-    def both(c, x, xs, *deps):
-        return [(c + j, mm(bank(c + j, 0, 128), w[:], ws[:], x, xs, *deps)) for j, (w, ws) in enumerate(((T.uq, T.us), (T.vq, T.vs)))]
-
-    def natural(ks, c, o, n, split):
-        (bu, ku), (bv, kv) = ks
-        ku = act(T.zu[:, o:o + n], bank(bu, c, c + n), F.Copy, 1.0, ku)
-        if split:
-            return ku, vec(v.tensor_copy, T.zv[:, o:o + n], bank(bv, c, c + n), deps=[kv])
-        return ku, act(T.zv[:, o:o + n], bank(bv, c, c + n), F.Copy, 1.0, kv)
-
-    p0 = both(4, T.rq[:, 0:128], T.rs[:, 0:128], k_u, k_v, ("arr0", arrive[0]))
-    p1 = both(6, T.rq[:, 128:256], T.rs[:, 128:256], ("arr1", arrive[1]))
-    best("o", 1, 0, 1)
-    last("o", 0, 0)
-    last("o", 0, 1)
-    last("o", 1, 0)
-    last("o", 1, 1)
-    k = vec(ts, T.pz[:], T.pl[:, 16:32], 0, SL, A.is_lt, A.mult, deps=[("pfg", 256)])
-    k_co = quant(T.oq[:], T.ow[:], T.tile[:, 4 * (SL - 128):4 * SL], k_t["o"])
-    k = vec(tt, T.pl[:, 16:32], T.pl[:, 16:32], T.pz[:], A.max, deps=[k])
-    k_pu = vec(v.tensor_copy, T.pu[:], T.pl[:], deps=[k])
-    po = both(0, T.oq[:], T.ow[:], k_co)
-    pm = both(2, T.rq[:, 192:320], T.rs[:, 192:320], ("arr2", arrive[2]))
-    natural(p0, 0, 128 * frm[0], 128, False)
-    natural(p1, 0, 128 * frm[1], 128, False)
-    natural(po, CAPP, CAPP * rank, CAPP, True)
-    k_zu2, k_zv = natural(pm, CAPP, CAPP * mate, CAPP, True)
-
-    need("cs_", k_pu, k_zu, k_zu2)
-    k_g = [done("cs_", s.activation(T.gu[:, 128 * h:128 * h + 128], T.zu[:].indirect(T.pu[:, 16 + 8 * h:24 + 8 * h]), F.Copy)) for h in (0, 1)]
-    need("cv", k_zv)
-    for h in (0, 1):
-        need("cv", k_g[h])
-        k = done("cv", v.tensor_tensor(T.yb[:, 128 * h:128 * h + 128], T.zv[:].indirect(T.pu[:, 8 * h:8 * h + 8]), T.gu[:, 128 * h:128 * h + 128], A.add))
-        need("sy", k)
+    for h in range(2):
+        need("sy", "y%d" % h)
         g.sync.dma_start(T.y[:, 128 * h:128 * h + 128], T.yb[:, 128 * h:128 * h + 128]).then_inc(T.sem["y%d" % h], 16)
-    g.wait_ge(T.sem.sent, sent)
-    need("sy", ("cs_", count["cs_"]), ("ct", count["ct"]), ("cg", count["cg"]), ("y0", 16), ("y1", 16))
+    need("sy", " ".join(order[q][-1] for q in order))
+    g.sync.wait_ge(T.sem.y0, 16)
+    g.sync.wait_ge(T.sem.y1, 16)

@@ -15,27 +15,28 @@ S0, H0, P0, RG = 0, J, 2 * J, 4 * J
 K = J + 2 * B - 1
 E0 = H0 + 2 * K - B - 1
 BIG, FAR = 1e29, 1e6
-PHI, LESS = float(2 ** 23 + 1), 1.0 - 2.0 ** -24
+PHI, LIFT = 2.0 ** 23, 2.0 ** 13
+M3 = 576
 
 
 def shift(m):
     return (2 ** m + 2) // 3
 
 
-CH = {"a": (0, 128), "b": (128, 128), "m": (256, 64), "o": (320, 64)}
-WORK = {"a0": 1, "a1": 3, "b0": 3, "b1": 3, "m0": 3, "m1": 3, "o0": 3, "o1": 3}
-
 ORDER = {
-    "cv": """one c0 pad0 r1 lm l6 pad1 r6 r r2 c1 sb qa0 nb b6 yy q qxa dd q2 qxb w fd qa1 ac ad ab qa2 of P0a qa3 f0 f1 od
-             S0 n0 P0b P1a P1b S1 L01 h3b P2 L02 P3 L03 S3 L11 L04 S2 L05 L12 Ba00 L06 L13 Ba01 L14 Ca00 L15 n1 Ca01 L16
-             sb00 sb01 Da00 Db00 Db01 Da01 sa10 sa11 Da10 Da11 sb10 sb11 qca Db10 Db11 sm0 sm1 qcb Dm00 Dm01 Dm10 Dm11 so0 qcm
-             so1 Do00 qu Do01 Do10 Do11 qv qco va pu vp vb y0 y1""",
-    "cs_": """ez1 e ne ez3 tc td pad2 pad3 ez0 ez2 zu zv tp h0a h0b h1a h1b h2a h2b h3a
-              Bb0 Aa0 Ab0 Bb1 Ba1 Cb0 Ab1 Aa1 Ca1 Bm0 Cb1 Am0 Cm0 Am1 Bm1 Cm1 Ao0 Bo0 Co0 Ao1 Bo1 Co1 ua ub up g0 g1""",
-    "ct": "z0a z0b z1a z1b z2a z2b z3a z3b Ua Ub Va Up Vp Vb",
-    "cg": "m6 m3",
+    "cv": """one c0 c1 pad0 pad1 ez0 ee2 ee0 ee1 sb qa0 nb qxa dd qxb qa1 fd w qa2 yy ab1 ac qa3 ab0 of1 P0a of0 S0 P0b f00 f01
+             f11 fx P1 S1 f21 L01 P2 f20 L02 P3 L03 S2 L11 L04 S3 L12 L05 B1:02 L13 L06 B0:02 L14 C1:02 L15 C0:02 L16 B2:02
+             D1:02 D0:02 C2:02 s3:02 s1:25 D2:02 D3:02 s0:25 qca D1:25 D0:25 s3:24 s2:24 s2:45 D3:24 D2:24 s3:45 D2:45 qcb
+             D3:45 s0:56 s1:56 qcm s2:56 s3:56 qu D1:56 D2:56 D3:56 pu qv qco vp vb va y0 y1""",
+    "cs_": """nl0 nl2 nl1 ej b6 e0 q q2 tc e1 td h0a ad h0b h1 h2 h3
+              B01:25 A01:02 A01:25 A23:02 C01:25 B3:02 C3:02 B23:25 C23:25 A23:25
+              B01:56 E0:56 A01:56 C01:56 E1:56 E2:56 C23:56 A23:56 B23:56 E3:56 ua ub up g0 g1""",
+    "ct": "z0a z0b z1 z2 z3 Ua Ub Up Vp Vb Va",
+    "cg": "m6 ez1 pad2 pad3 ez3 ez2 m3 zu zv tp m4",
 }
-LOADS = "x:a a:0 x:b a:1 a:2 a:3"
+SPANS = [(0, 2), (2, 5), (5, 6)]
+LOADS = "l:n l:o x:a a:0 x:b a:1 a:2 a:3 u:0 v:0"
+ON_SCALAR = ("l:n", "a:0")
 
 SCRATCH = {
     "xb": ("sbuf", [128, 2048], "bfloat16"), "ab": ("sbuf", [128, 2048], "bfloat16"),
@@ -49,24 +50,20 @@ SCRATCH = {
     "mq": ("sbuf", [128, 192], "float8_e4m3fn_x4"), "ms": ("sbuf", [128, 384], "uint8"),
     "win": ("sbuf", [128, 2 * RG], "bfloat16"),
     "tile": ("sbuf", [128, 4 * (SL + CAPP)], "bfloat16"),
-    "ones": ("sbuf", [128, ST], "bfloat16"), "m6": ("sbuf", [128, ST], "bfloat16"),
-    "m2": ("sbuf", [128, 512], "bfloat16"), "m3": ("sbuf", [128, 384], "bfloat16"), "m4": ("sbuf", [128, 512], "bfloat16"),
-    "ll": ("sbuf", [128, 4 * NS], "int32"), "qq": ("sbuf", [128, 6 * NS], "float32"),
-    "l6": ("sbuf", [128, 2 * NS], "int32"), "sb": ("sbuf", [128, 2 * NS], "int32"), "ee": ("sbuf", [128, 2 * NS], "float32"),
-    "dd": ("sbuf", [128, 2 * NS], "float32"), "sg": ("sbuf", [128, 2 * NS], "float32"), "fd": ("sbuf", [128, 2 * NS], "float32"),
-    "d0": ("sbuf", [128, 6 * NS], "float32"), "d1": ("sbuf", [128, 6 * NS], "float32"),
-    "of": ("sbuf", [128, 12 * NS], "float32"),
-    "o1": ("sbuf", [128, 9, 32], "uint16"), "o2": ("sbuf", [128, 6, 16], "uint16"), "od": ("sbuf", [128, NS], "uint16"),
+    "ones": ("sbuf", [128, M3], "bfloat16"), "m6": ("sbuf", [128, ST], "bfloat16"), "m3": ("sbuf", [128, M3], "bfloat16"),
+    "ll": ("sbuf", [128, 2, NS], "int32"), "xf": ("sbuf", [128, 4, NS], "float32"), "qq": ("sbuf", [128, 4 * NS], "float32"),
+    "sb": ("sbuf", [128, 2 * NS], "int32"), "ee": ("sbuf", [128, 2 * NS], "float32"),
+    "dd": ("sbuf", [128, 2 * NS], "float32"), "fd": ("sbuf", [128, 2 * NS], "float32"), "sg": ("sbuf", [128, 2 * NS], "float32"),
+    "dq": ("sbuf", [128, 12 * NS + 3], "float32"),
+    "of": ("sbuf", [128, 4, 3 * NS], "float32"), "od": ("sbuf", [128, NS], "uint16"), "oo": ("sbuf", [128, 3, 2 * NS], "uint16"),
+    "g0": ("sbuf", [128, 8 * SL], "bfloat16"), "g1": ("sbuf", [128, 8 * SL], "bfloat16"), "m4": ("sbuf", [128, 512], "bfloat16"),
     "pl": ("sbuf", [128, 32], "int32"), "pu": ("sbuf", [128, 32], "uint16"),
-    "zu": ("sbuf", [128, SL + 1], "float32"), "zv": ("sbuf", [128, SL + 1], "float32"),
+    "zu": ("sbuf", [128, SL + 1], "float32"), "zv": ("sbuf", [128, SL + 1], "float32"), "zw": ("sbuf", [128, SL + 1], "float32"),
     "gu": ("sbuf", [128, P], "float32"), "yb": ("sbuf", [128, P], "float32"),
     "zp": ("psum", [128, 2048], "float32"), "pp": ("psum", [128, 2048], "float32"),
 }
-for _u, _w in WORK.items():
-    SCRATCH["g" + _u[0]] = ("sbuf", [128, 2 * (WORK[_u[0] + "0"] + WORK[_u[0] + "1"]) * CH[_u[0]][1]], "bfloat16")
-    SCRATCH["s" + _u] = ("sbuf", [128, 2 * _w * CH[_u[0]][1]], "bfloat16")
-    SCRATCH["c" + _u] = ("sbuf", [128, 2 * CH[_u[0]][1]], "bfloat16")
-SEMAPHORES = ["cv", "cs_", "ct", "cg", "lists", "uv", "pfg", "y0", "y1", "arr0", "arr1", "arr2", "sent"] + LOADS.replace(":", "").split()
+SCRATCH.update({"t%d" % i: ("sbuf", [128, 8 * SL], "bfloat16") for i in range(2)})
+SEMAPHORES = ["cv", "cs_", "ct", "cg", "lists", "pfg", "y0", "y1", "arr0", "arr1", "arr2", "sent"] + [w.replace(":", "") for w in LOADS.split() if w[0] != "l"]
 
 
 def rank_program(g, core, T, topo):
@@ -79,13 +76,16 @@ def rank_program(g, core, T, topo):
     v, s, t = g.vector, g.scalar, g.tensor
     ts, tt, scan = v.tensor_scalar, v.tensor_tensor, v.tensor_tensor_scan
     pair, mate, odd = rank // 2, rank ^ 1, rank % 2
-    to = {"a": (pair + 1) % 3, "b": (pair + 2) % 3}
-    frm = {"a": (pair + 2) % 3, "b": (pair + 1) % 3}
     eng = topo.engines(core, T.cores[mate])
 
+    pairs = [(pair + k) % 3 for k in ((1, 2, 0) if odd else (0, 2, 1))]
+
+    def cols(c0, c1):
+        return (4 * c0, 4 * c1) if odd else (NS - 4 * c1, NS - 4 * c0)
+
     when = {name: [(q, k + 1)] for q in order for k, name in enumerate(order[q])}
-    when.update({"in": [("lists", 32)], "uv": [("uv", 32)], "pfg": [("pfg", 256)]})
-    when.update({"in" + x.replace(":", ""): [(x.replace(":", ""), 16)] for x in LOADS.split()})
+    when.update({"in": [("lists", 32)], "pfg": [("pfg", 256)]})
+    when.update({"in" + x[0] + c: [(x.replace(":", ""), 16)] for x in LOADS.split() for c in x[2:]})
     when.update({"arr" + h: [("arr%d" % k, n * len(eng))] for k, (h, n) in enumerate((("a", 2), ("b", 2), ("m", 1)))})
     seen = {q: {} for q in que}
     calls = {}
@@ -113,16 +113,24 @@ def rank_program(g, core, T, topo):
     def zero(name, out, n):
         if name in order["cv"]:
             call(name, "", v.memset, out, 0.0)
+        elif name in order["cg"]:
+            call(name, "one", g.affine_select, out, T.ones[:, 0:n], [[0, n]], A.is_gt, 0.0, 0, 0)
         else:
             call(name, "one", s.activation, out, T.ones[:, 0:n], F.Copy, scale=0.0)
 
-    s.dma_start(T.ll[:, 0:NS], T.ln[:]).then_inc(T.sem.lists, 16)
-    g.sync.dma_start(T.ll[:, 2 * NS:3 * NS], T.lo[:]).then_inc(T.sem.lists, 16)
-    for k, (x, c) in enumerate(w.split(":") for w in LOADS.split()):
-        a, b = (4 * CUT[c][0], 4 * CUT[c][1]) if x == "x" else (512 * int(c), 512 * int(c) + 512)
-        (s if k == 1 else g.sync).dma_start(T[x + "b"][:, a:b], T[x][:, a:b]).then_inc(T.sem[x + c], 16)
-    g.sync.dma_start(T.ub[:], T.u[:]).then_inc(T.sem.uv, 16)
-    g.sync.dma_start(T.vb[:], T.v[:]).then_inc(T.sem.uv, 16)
+    def line(name, reads, out, src, c, b):
+        if name in order["cv"]:
+            call(name, reads, ts, out, src, c, b, A.mult, A.add)
+        else:
+            call(name, reads, s.activation, out, src, F.Identity, bias=b, scale=c)
+
+    for w in LOADS.split():
+        q, (x, c) = s if w in ON_SCALAR else g.sync, w.split(":")
+        if x == "l":
+            q.dma_start(T.ll[:, "no".index(c), :], T[x + c][:]).then_inc(T.sem.lists, 16)
+            continue
+        a, b = (4 * CUT[c][0], 4 * CUT[c][1]) if x == "x" else (512 * int(c[0]), 512 * int(c[-1]) + 512)
+        q.dma_start(T[x + "b"][:, a:b], T[x][:, a:b]).then_inc(T.sem[x + c], 16)
     for k in range(8):
         g.sync.dma_start(T.pl[16 * k:16 * k + 16, 0:16], T.pf[:]).then_inc(T.sem.pfg, 16)
         g.sync.dma_start(T.pl[16 * k:16 * k + 16, 16:32], T.pg[:]).then_inc(T.sem.pfg, 16)
@@ -130,15 +138,18 @@ def rank_program(g, core, T, topo):
     def at(i):
         return (i // 2) * RG + (i % 2) * ST
 
+    H = 3 * NS
     call("one", "", v.memset, T.ones[:], 1.0)
-    call("c0", "", v.memset, T.d0[:, 0::3], FAR)
-    call("c1", "", v.memset, T.d1[:, 2::3], FAR)
+    D1, D0R = H + 1, 3 * H + 3
+    call("c0", "", v.memset, T.dq[:, 0:D1 + H:3], FAR)
+    call("c1", "", v.memset, T.dq[:, D1 + H + 2::3], -FAR)
     for i in range(4):
         zero("pad%d" % i, T.win[:, at(i) + H0 + T_COLS:at(i) + H0 + ST], ST - T_COLS)
     zero("zu", T.zu[:, 0:1], 1)
     zero("zv", T.zv[:, 0:1], 1)
-    zero("tp", T.tile[:, 4 * SL:4 * (SL + CAPP)], 4 * CAPP)
-    for b, n in ((B, ST), (2, 512), (3, 384), (4, 512)):
+    t0 = 0 if odd else CAPP
+    zero("tp", T.tile[:, 4 * SL * odd:4 * (SL * odd + CAPP)], 4 * CAPP)
+    for b, n in ((B, ST), (3, M3), (4, 512)):
         call("m%d" % b, "one", g.affine_select, T["m%d" % b][:], T.ones[:, 0:n], [[0, n // b], [1, b]], A.is_gt, 0.0, 0, 0)
     lead, tail = E0 + shift(LV), E0 + shift(LV) + B * (NB + USED - 2 ** LV) + 1
     for p in range(2):
@@ -146,57 +157,52 @@ def rank_program(g, core, T, topo):
             zero("ez%d" % (2 * p + k), T.win[:, p * RG + a:p * RG + b], b - a)
 
     lo_, hi_ = slice(0, NS), slice(NS, 2 * NS)
-    n_, L_, R_, LR, RL = T.ll[:, lo_], T.ll[:, 2 * NS:3 * NS], T.ll[:, 3 * NS:4 * NS], T.ll[:, 2 * NS:4 * NS], T.ll[:, NS:3 * NS]
-    lm_, r1_, nb_, q_, q2_, w_ = (T.qq[:, k * NS:(k + 1) * NS] for k in range(6))
-    b6_, yy_ = T.d1[:, 0::3], T.d1[:, 1::3]
-    tc_, td_, ac_, ad_ = T.d0[:, 1:3 * NS:3], T.d0[:, 3 * NS + 1::3], T.d0[:, 2:3 * NS:3], T.d0[:, 3 * NS + 2::3]
-    base = -B - 0.25 + (0 if "tc" in order["cv"] else 2 * K)
-    call("r1", "in", tt, r1_, L_, n_, A.add)
-    call("lm", "in", ts, lm_, n_, -1, None, A.add)
-    call("l6", "in", ts, T.l6[:, lo_], L_, B, 683, A.add, A.mult)
-    call("r6", "r1", ts, T.l6[:, hi_], r1_, -1, 683, A.add, A.mult)
-    call("r", "lm", tt, R_, L_, lm_, A.add)
-    call("r2", "r1", ts, T.ll[:, hi_], r1_, 1, None, A.add)
-    call("e", "lm", s.activation, T.ee[:, hi_], lm_, F.Sign)
-    call("ne", "lm", s.activation, T.ee[:, lo_], lm_, F.Sign, scale=-1.0)
-    call("sb", "l6 r6", ts, T.sb[:], T.l6[:], 12, None, A.arith_shift_right)
-    call("yy", "r e ne", tt, yy_, T.ee[:], LR, A.subtract)
-    call("nb", "sb", tt, nb_, T.sb[:, hi_], T.sb[:, lo_], A.subtract)
-    call("b6", "sb", ts, b6_, T.sb[:], -B, base, A.mult, A.subtract)
-    if "q" in order["cv"]:
-        call("q", "nb", ts, q_, nb_, 0, PHI, A.max, A.mult)
-    else:
-        call("q", "nb", s.activation, q_, nb_, F.Relu, scale=PHI)
-    if "q2" in order["cv"]:
-        call("q2", "q", ts, q2_, q_, LESS, None, A.mult)
-    else:
-        call("q2", "q", s.activation, q2_, q_, F.Copy, scale=LESS)
-    call("w", "q q2", tt, w_, q_, q2_, A.subtract)
-    call("dd", "b6 r2", tt, T.dd[:], b6_, RL, A.add)
-    call("sg", "dd", s.activation, T.sg[:], T.dd[:], F.Sign, bias=base - 0.25)
+    nb_, q_, q2_, w_ = (T.qq[:, k * NS:(k + 1) * NS] for k in range(4))
+    b6_, yy_, x_ = T.dq[:, D1:D1 + 2 * H:3], T.dq[:, D1 + 1:D1 + 2 * H:3], T.xf[:, 1:3, :]
+    G0 = E0 - H0
+    for k, q in enumerate(pairs):
+        o, a = 8 * k, 8 * q
+        line("nl%d" % k, "in", T.xf[:, 0:2, o:o + 8], T.ll[:, :, a:a + 8], -1.0, -0.5)
+        call("ee%d" % k, "in", tt, T.xf[:, 2, o:o + 8], T.ll[:, 0, a:a + 8], T.ll[:, 1, a:a + 8], A.add)
+    alias("nl", "nl0", "nl1", "nl2")
+    alias("ee", "ee0", "ee1", "ee2")
+    call("sb", "nl ee", ts, T.sb[:], x_, -3.25, 1 / B, A.add, A.mult)
+    call("nb", "sb", tt, nb_, T.sb[:, hi_], T.sb[:, lo_], A.add)
+    line("b6", "sb", b6_, T.sb[:], 1.0 * B, 0.0)
+    call("dd", "b6", tt, T.dd[:], b6_, T.xf[:, 2:0:-1, :], A.add)
+    call("sg", "dd", s.activation, T.sg[:], T.dd[:], F.Sign, bias=0.75)
     if "sg" in when:
-        call("fd", "sg", s.activation, T.fd[:], T.sg[:], F.Identity, bias=-J / 2, scale=J / 2)
+        line("fd", "sg", T.fd[:], T.sg[:], -J / 2, -J / 2)
     else:
-        call("fd", "dd", ts, T.fd[:], T.dd[:], 0.25 - base, -J, A.is_le, A.mult)
-    call("ab", "fd r", tt, T.of[:, 2:6 * NS:3], T.fd[:], LR, A.subtract)
-    for name, out in (("tc", tc_), ("td", td_)):
-        if name in order["cv"]:
-            call(name, "nb", ts, out, nb_, 2, -K, A.min, A.mult)
-        else:
-            call(name, "nb", s.activation, out, nb_, F.Relu, bias=2.0 * K, scale=-1.0 * K)
-    for name, out, c in (("ac", ac_, -1 / 3), ("ad", ad_, B - 1 / 3)):
-        if name in order["cv"]:
-            call(name, "w", ts, out, w_, c, None, A.mult)
-        else:
-            call(name, "w", s.activation, out, w_, F.Copy, scale=c)
-    if "e" in order["cv"]:
-        call("e", "in", ts, T.ee[:, hi_], n_, -1, 1, A.add, A.min)
-        call("ne", "lm", ts, T.ee[:, lo_], lm_, -1, -1, A.mult, A.max)
-    call("of", "c0 c1 b6 yy tc td ac ad", scan, T.of[:, 6 * NS:12 * NS], T.d0[:], T.d1[:], 0.0, A.add, A.min)
-    for i in range(4):
-        call("f%d" % i, "ab of", ts, T.o1[:, :, 8 * i:8 * i + 8], T.of[:, 2:9 * NS:3], -1, at(i), A.mult, A.add)
-        call("n%d" % i, "f%d" % i, v.tensor_copy, T.o2[:, :, 4 * i:4 * i + 4], T.o1[:, pair::3, 8 * i:8 * i + 8])
-    call("od", "of", ts, T.od[:], T.of[:, 9 * NS + 2::3], -1, None, A.mult)
+        call("fd", "dd", ts, T.fd[:], T.dd[:], -0.75, -J, A.is_ge, A.mult)
+    call("ab0", "fd", tt, T.of[:, 0, 2::3], T.xf[:, 1, :], T.fd[:, lo_], A.subtract)
+    line("ej", "ee", T.xf[:, 3, :], T.xf[:, 2, :], 1.0, -1.0 * J)
+    call("ab1", "fd ej", tt, T.of[:, 1, 2::3], T.fd[:, hi_], T.xf[:, 3, :], A.subtract)
+    line("e0", "nl", T.ee[:, lo_], T.xf[:, 0, :], 1 / 3, G0 + 1.25)
+    line("e1", "nl", T.ee[:, hi_], T.xf[:, 0, :], 1 / 3, -G0 - 0.75)
+    call("yy", "ee e0 e1", tt, yy_, T.ee[:], x_, A.add)
+    call("q", "nb", s.activation, q_, nb_, F.Relu, bias=LIFT, scale=PHI)
+    call("q2", "nb", s.activation, q2_, nb_, F.Relu, bias=LIFT - 2.0 ** -11, scale=PHI - 0.5)
+    call("w", "q q2", tt, w_, q_, q2_, A.subtract)
+    call("tc", "nb", s.activation, T.dq[:, 1:H:3], nb_, F.Relu, bias=2.0 * K, scale=-1.0 * K)
+    line("td", "tc", T.dq[:, D0R + 1::3], T.dq[:, 1:H:3], -1.0, 0.0)
+    line("ac", "w", T.dq[:, 2:H:3], w_, -1 / 3, J - G0 - 1.0)
+    line("ad", "w", T.dq[:, D0R + 2::3], w_, 1 / 3 - B, G0 + 0.25)
+    call("of0", "c0 b6 yy tc ac", scan, T.of[:, 2, :], T.dq[:, 0:H], T.dq[:, D1:D1 + H], 0.0, A.add, A.min)
+    call("of1", "c1 b6 yy td ad", scan, T.of[:, 3, :], T.dq[:, D0R:], T.dq[:, D1 + H:D1 + 2 * H], 0.0, A.add, A.max)
+    left = 1 - odd
+    wide = [4 * (b - a) for a, b in SPANS]
+    begin = {left: 0, 1 - left: 2 * wide[left], 2: 2 * (wide[0] + wide[1])}
+
+    def offsets(name, o, a, b, j):
+        call(name, "ab0 ab1 of0", ts, T.oo[:, :, o:o + b - a], T.of[:, 0:3, 3 * a + 2:3 * b:3], -1, J - 0.75 + ST * j, A.mult, A.add)
+
+    offsets("f00", wide[left], *cols(0, SPANS[1][1]), 0)
+    alias("f10", "f00")
+    offsets("f20", begin[2], *cols(*SPANS[2]), 0)
+    for u, span in enumerate(SPANS):
+        offsets("f%d1" % u, begin[u] + wide[u] * (u != left), *cols(*span), 1)
+    copy("fx", "of1", T.od[:], T.of[:, 3, 2::3])
 
     def bank(k, a, b):
         return T.zp[:, 512 * k + a:512 * k + b] if k < 4 else T.pp[:, 512 * (k - 4) + a:512 * (k - 4) + b]
@@ -237,78 +243,79 @@ def rank_program(g, core, T, topo):
             b, o = a + B * 2 ** (m - 1), p * RG + E0 + shift(m)
             call("L%d%d" % (p, m), "L%d%d" % (p, m - 1), scan, T.win[:, o:o + n:B], T.win[:, a:a + n:B], T.win[:, b:b + n:B], BIG, A.min, A.max)
 
-    WIN = [(S0, P0), (H0, P0 + J), (H0, RG), (H0, RG)]
-    for u, w in WORK.items():
-        h, p = u[0], int(u[1])
-        (c, n), who = CH[h], {"m": mate, "o": rank}.get(h)
-        kind = "f" if h in to else "n"
-        lists = "%s0 %s1" % (kind, kind)
-        tables = ["S%d S%d" % (2 * p, 2 * p + 1), "P%d P%d" % (2 * p, 2 * p + 1), "L%d%d" % (p, LV), "L%d%d" % (p, LV)]
-        gat, top, third = T["g" + h], T["s" + u], T["c" + u]
-        g0 = 2 * p * WORK[h + "0"] * n
+    WIN = {"A": (S0, P0), "B": (H0, P0 + J), "C": (H0, RG)}
+    named = {x: (x[0], [int(i) for i in x[1:-3]], int(x[-2]), int(x[-1])) for q in ("cv", "cs_") for x in order[q] if ":" in x}
 
-        def part(e, j0, j1):
-            a, b = WIN[e]
-            off = T.o1[:, 3 * e + to[h], 8 * j0:8 * j1] if h in to else T.o2[:, 2 * e + who % 2, 4 * j0:4 * j1]
-            if j1 > 2:
-                return T.win[:, a:RG + b].indirect(off)
-            return T.win[:, p * RG + a:p * RG + b].indirect(off)
+    def over(kinds, i, c0, c1, queue=None):
+        return " ".join(x for x, (kind, its, a, b) in named.items()
+                        if kind in kinds and set(its) & set(i) and a < c1 and c0 < b and (queue is None or x in order[queue]))
 
-        for e in range(w):
-            x = "ABCE"[e]
-            call(x + u, lists + " " + tables[e], s.activation, gat[:, g0 + e:g0 + 2 * w * n:w], part(e, 0, 2), F.Copy)
-            if p and x + h in when:
-                call(x + h, "%s %s2 %s3 S0 S1 L0%d %s" % (lists, kind, kind, LV, tables[e]), s.activation, gat[:, e:4 * w * n:w], part(e, 0, 4), F.Copy)
-            alias(x + u, x + h)
-        got = "m%d " % w + " ".join("ABCE"[e] + u for e in range(w))
-        before = ["", "A", "s" if w == 2 else "B", "s" if w == 3 else "C"]
-
-        def held(e, a, b):
-            if e == w:
-                return top[:, w * a + w - 1:w * b:w] if w > 1 else gat[:, g0 + a:g0 + b]
-            return (top if e == 2 else third)[:, a:b]
-
-        for x in "sABC":
-            alias(x + u, x + u + "0", x + u + "1")
-            alias(x + u + "0", x + u)
-            alias(x + u + "1", x + u)
-        for x, (j0, j1) in {"": (0, 2), "0": (0, 1), "1": (1, 2)}.items():
-            a, b = n * j0, n * j1
-            if w > 1 and w * (b - a) <= SCRATCH["m%d" % w][1][1]:
-                call("s" + u + x, got, scan, top[:, w * a:w * b], T["m%d" % w][:, 0:w * (b - a)], gat[:, g0 + w * a:g0 + w * b], 0.0, A.mult, A.max)
-            for e in range(w, 3):
-                call("ABC"[e] + u + x, "%s %s %s" % (lists, tables[e], before[e] + u + x), tt, held(e + 1, a, b), part(e, j0, j1), held(e, a, b), A.max)
-        for j in range(2):
-            name, out = "D%s%d" % (u, j), T.tile[:, 4 * c + 2 * p + j:4 * (c + n):4]
-            if w < 4:
-                o = 8 * to[h] if h in to else 4 * who
-                src = T.win[:, at(2 * p + j) + H0:p * RG + RG].indirect(T.od[:, o:o + n // 16])
-                call(name, "od %s%s%d" % (before[3], u, j), tt, out, src, held(3, n * j, n * j + n), A.max)
+    for name, (x, its, c0, c1) in named.items():
+        i, (k0, k1) = its[0], cols(c0, c1)
+        p, j = i // 2, i % 2
+        w = 4 if over("E", its, c0, c1) else 3
+        ta, tb, last = 4 * (t0 + 16 * k0), 4 * (t0 + 16 * k1), T.win[:, at(i) + H0:p * RG + RG].indirect(T.od[:, k0:k1])
+        u = [u for u, (a, b) in enumerate(SPANS) if a <= c0 and c1 <= b][0]
+        u0, u1 = cols(*SPANS[u])
+        a = k0 - u0 + wide[u] * (len(its) == 1 and j != (u == left))
+        b = a + len(its) * (k1 - k0)
+        gat, top, ga, gb = T["g%d" % p], T["t%d" % p], 128 * u0 + 16 * w * a, 128 * u0 + 16 * w * b
+        pa, pb = ga, gb
+        if x == "D" and w == 4:
+            copy(name, over("s", [0, i], c0, c1), T.tile[:, ta + i:tb:4], top[:, pa + 3:pb:4])
+            continue
+        if x == "D":
+            reads = "fx L%d%d %s %s" % (p, LV, over("s", its, c0, c1), over("C", its, c0, c1, "cv"))
+            call(name, reads, tt, T.tile[:, ta + i:tb:4], last, top[:, pa + 2:pb:3], A.max)
+            continue
+        if x == "s":
+            reads, mask = "m%d %s" % (w, over("ABCE", its, c0, c1)), T["m%d" % w][:, 0:gb - ga]
+            if w == 4 and i == 0:
+                call(name, reads, scan, T.tile[:, tb - 1:ta - 1:-1], mask, gat[:, gb - 1:ga - 1 if ga else None:-1], 0.0, A.mult, A.max)
             else:
-                copy(name, "s%s%d" % (u, j), out, held(4, n * j, n * j + n))
-    for h in CH:
-        alias("D" + h, *["D%s%d%d" % (h, p, j) for p in range(2) for j in range(2)])
-    place = {"a": 128 * odd, "b": 128 + 128 * odd, "m": 256 - 256 * odd}
-    for h, (c, reads) in {"a": (0, "Da"), "b": (128, "Db"), "m": (192, "Db Dm")}.items():
-        o = place[h]
-        call("qc" + h, reads, v.quantize_mx, T.cq[:, o:o + 128], T.cs[:, o:o + 128], T.tile[:, 4 * c:4 * c + 512])
-    c, oq, os_ = (320, CAPP, 256) if odd else (256, 0, 0)
-    call("qco", "Dm Do tp", v.quantize_mx, T.mq[:, oq:oq + 128], T.ms[:, os_:os_ + 128], T.tile[:, 4 * c:4 * c + 512])
+                call(name, reads, scan, top[:, pa:pb], mask, gat[:, ga:gb], 0.0, A.mult, A.max)
+            continue
+        if x == "E":
+            call(name, "fx L%d%d" % (p, LV), s.activation, gat[:, ga + 3:gb:4], last, F.Copy)
+            continue
+        e = "ABC".index(x)
+        o = begin[u] + (k0 - u0 + wide[u] * (u == left) if len(its) == 1 else 0)
+        src = T.win[:, at(i) + WIN[x][0]:p * RG + WIN[x][1]].indirect(T.oo[:, e, o:o + b - a])
+        reads = " ".join("f%d%d" % (u, y) for y in range(len(its))) + " "
+        reads += {"A": "S%d S%d" % (2 * p, 2 * p + 1), "B": "P%d P%d" % (2 * p, 2 * p + 1), "C": "L%d%d" % (p, LV)}[x]
+        if name in order["cs_"]:
+            call(name, reads, s.activation, gat[:, ga + e:gb:w], src, F.Copy)
+        else:
+            held = gat[:, ga:gb:3] if e == 1 else top[:, pa + 1:pb:3]
+            call(name, reads + " " + over("ABC"[e - 1], its, c0, c1), tt, top[:, pa + e:pb:3], src, held, A.max)
 
-    call("qu", "uv", v.quantize_mx, T.uq[:], T.us[:], T.ub[:])
-    call("qv", "uv", v.quantize_mx, T.vq[:], T.vs[:], T.vb[:])
+    place = {"a": 128 * odd, "b": 128 + 128 * odd, "m": 256 - 256 * odd}
+    for h, (c0, c1) in {"a": (0, 2), "b": (2, 4), "m": (3, 5)}.items():
+        o, c = place[h], t0 + 16 * cols(c0, c1)[0]
+        call("qc" + h, over("D", range(4), c0, c1), v.quantize_mx, T.cq[:, o:o + 128], T.cs[:, o:o + 128], T.tile[:, 4 * c:4 * c + 512])
+    c, oq, os_ = (SL - CAPP, CAPP, 256) if odd else (0, 0, 0)
+    call("qco", "tp " + over("Ds", range(4), 5, 6), v.quantize_mx, T.mq[:, oq:oq + 128], T.ms[:, os_:os_ + 128], T.tile[:, 4 * c:4 * c + 512])
+
+    call("qu", "inu0", v.quantize_mx, T.uq[:], T.us[:], T.ub[:])
+    call("qv", "inv0", v.quantize_mx, T.vq[:], T.vs[:], T.vb[:])
     call("pu", "pfg", ts, T.pu[:], T.pl[:], 1, None, A.add)
     oq, os_ = (0, 192) if odd else (CAPP, CAPP)
-    second = {"a": (T.rq[:, 0:128], T.rs[:, 0:128], "arra", frm["a"]), "b": (T.rq[:, 128:256], T.rs[:, 128:256], "arrb", frm["b"]),
-              "p": (T.mq[:, oq:oq + 128], T.ms[:, os_:os_ + 128], "qco arrm", pair)}
-    for k, (h, (x, xs, reads, o)) in enumerate(second.items()):
+    second = {"a": (T.rq[:, 0:128], T.rs[:, 0:128], "arra"), "b": (T.rq[:, 128:256], T.rs[:, 128:256], "arrb"),
+              "p": (T.mq[:, oq:oq + 128], T.ms[:, os_:os_ + 128], "qco arrm")}
+    for k, (h, (x, xs, reads)) in enumerate(second.items()):
         for j, (name, w, ws, out) in enumerate((("u", T.uq, T.us, T.zu), ("v", T.vq, T.vs, T.zv))):
-            ps = bank(2 * k + j, 0, 128)
-            call(name.upper() + h, "h0 h1 h2 h3 q%s %s" % (name, reads), t.matmul_mx, ps, w[:], ws[:], x, xs, True, True)
-            copy(name + h, name.upper() + h, out[:, 128 * o + 1:128 * o + 129], ps)
+            call(name.upper() + h, "h0 h1 h2 h3 q%s %s" % (name, reads), t.matmul_mx, bank(2 * k + j, 0, 128), w[:], ws[:], x, xs, True, True)
+            o = 128 * ((pair + 2 - k) % 3) + 1
+            copy(name + h, name.upper() + h, out[:, o:o + 128], bank(2 * k + j, 0, 128))
+        if h != "p":
+            copy("w" + h, "u" + h, T.zw[:, o:o + 128], bank(2 * k, 0, 128))
+    call("Wp", "h0 h1 h2 h3 qu " + reads, t.matmul_mx, bank(6, 0, 128), T.uq[:], T.us[:], x, xs, True, True)
+    copy("wp", "Wp", T.zw[:, o:o + 128], bank(6, 0, 128))
+    zero("zw", T.zw[:, 0:1], 1)
     for h in range(2):
         a, b = 128 * h, 128 * h + 128
-        call("g%d" % h, "pu zu ua ub up", s.activation, T.gu[:, a:b], T.zu[:].indirect(T.pu[:, 16 + 8 * h:24 + 8 * h]), F.Copy)
+        x = "w" if "g%d" % h in order["cv"] and "wp" in when else "u"
+        copy("g%d" % h, "pu z%s %sa %sb %sp" % ((x,) * 4), T.gu[:, a:b], T["z" + x][:].indirect(T.pu[:, 16 + 8 * h:24 + 8 * h]))
         call("y%d" % h, "pu zv va vb vp g%d" % h, tt, T.yb[:, a:b], T.zv[:].indirect(T.pu[:, 8 * h:8 * h + 8]), T.gu[:, a:b], A.add)
 
     for q in order:
@@ -325,19 +332,19 @@ def rank_program(g, core, T, topo):
     for k, h in enumerate("ab"):
         need("cg", "qc" + h)
         b = 128 * k + CAPP * odd
-        ds = [(2 * to[h] + j, place[h] + CAPP * j) for j in range(2)]
+        ds = [(2 * ((pair + 1 + k) % 3) + j, place[h] + CAPP * j) for j in range(2)]
         g.remote_dma_fused([transfer(r, half[j], T.cq[:, c:c + CAPP].bitcast(dt.uint8), T.rq[:, b:b + CAPP].bitcast(dt.uint8), k)
                             for j, (r, c) in enumerate(ds)], local_sem=T.sem.sent)
         g.remote_dma_fused([transfer(r, half[j], T.cs[:, c:c + CAPP], T.rs[:, b:b + CAPP], k) for j, (r, c) in enumerate(ds)], local_sem=T.sem.sent)
     need("cg", "qca qcb qcm")
-    c, b, a, o = place["m"] + CAPP, 128 * odd, 128 - CAPP * odd, 128 * odd
+    c, b, o = place["m"] + CAPP * odd, 128 * odd, 128 * odd
     g.remote_dma_fused([transfer(mate, half[0], T.cq[:, c:c + CAPP].bitcast(dt.uint8), T.mq[:, b:b + CAPP].bitcast(dt.uint8), 2),
-                        transfer(mate, half[1], T.cs[:, a:a + 256], T.ms[:, o:o + 256], 2)], local_sem=T.sem.sent)
+                        transfer(mate, half[1], T.cs[:, CAPP:CAPP + 256], T.ms[:, o:o + 256], 2)], local_sem=T.sem.sent)
     g.wait_ge(T.sem.sent, 5 * len(eng))
 
-    for h in range(2):
-        need("sy", "y%d" % h)
-        g.sync.dma_start(T.y[:, 128 * h:128 * h + 128], T.yb[:, 128 * h:128 * h + 128]).then_inc(T.sem["y%d" % h], 16)
+    for h, q in enumerate(("sy", "cs_")):
+        need(q, "y%d" % h)
+        que[q].dma_start(T.y[:, 128 * h:128 * h + 128], T.yb[:, 128 * h:128 * h + 128]).then_inc(T.sem["y%d" % h], 16)
     need("sy", " ".join(order[q][-1] for q in order))
     g.sync.wait_ge(T.sem.y0, 16)
     g.sync.wait_ge(T.sem.y1, 16)

from concourse.bass import DstId, RemoteDMATransfer
from concourse.mybir import dt, AluOpType, ActivationFunctionType

N, T_COLS, CAPP, P = 6, 512, 64, 256
SL = N * CAPP
NS = SL // 16
B = 6
ST = 528
NB, USED = ST // B, 86
LV = 6
XC = 43 * B
CUT = {"a": (0, XC), "b": (XC, T_COLS), "": (0, T_COLS)}
J = 2 * ST
S0, H0, P0, RG = 0, J, 2 * J, 4 * J
K = J + 2 * B - 1
E0 = H0 + 2 * K - B - 1
BIG, FAR = 1e29, 1e6
PHI, LIFT = 2.0 ** 23, 2.0 ** 13
M3 = 576


def shift(m):
    return (2 ** m + 2) // 3


ORDER = {
    "cv": """one c0 c1 pad0 pad1 ez0 ee2 ee0 ee1 sb qa0 nb qxa dd qxb qa1 fd w qa2 yy ab1 ac qa3 ab0 of1 P0a of0 S0 P0b f00 f01
             f11 fx P1 S1 f21 L01 P2 f20 L02 P3 L03 S2 L11 L04 S3 L12 L05 B1:02 L13 L06 B0:02 L14 C1:02 L15 C0:02 L16 B2:02
             D1:02 D0:02 C2:02 s3:02 s1:25 D2:02 D3:02 s0:25 qca D1:25 D0:25 s3:24 s2:24 s2:45 D3:24 D2:24 s3:45 D2:45 qcb
             D3:45 s0:56 s1:56 qcm s2:56 s3:56 qu D1:56 D2:56 D3:56 pu qv qco vp vb va y0 y1""",
    "cs_": """nl0 nl2 nl1 ej b6 e0 q q2 tc e1 td h0a ad h0b h1 h2 h3
              B01:25 A01:02 A01:25 A23:02 C01:25 B3:02 C3:02 B23:25 C23:25 A23:25
              B01:56 E0:56 A01:56 C01:56 E1:56 E2:56 C23:56 A23:56 B23:56 E3:56 ua ub up g0 g1""",
    "ct": "z0a z0b z1 z2 z3 Ua Ub Up Vp Vb Va",
    "cg": "m6 ez1 pad2 pad3 ez3 ez2 m3 zu zv tp m4",
}
SPANS = [(0, 2), (2, 5), (5, 6)]
LOADS = "l:n l:o x:a a:0 x:b a:1 a:2 a:3 u:0 v:0"
ON_SCALAR = ("l:n", "a:0")

SCRATCH = {
    "xb": ("sbuf", [128, 2048], "bfloat16"), "ab": ("sbuf", [128, 2048], "bfloat16"),
    "ub": ("sbuf", [128, 512], "bfloat16"), "vb": ("sbuf", [128, 512], "bfloat16"),
    "xq": ("sbuf", [128, 512], "float8_e4m3fn_x4"), "xs": ("sbuf", [128, 512], "uint8"),
    "aq": ("sbuf", [128, 512], "float8_e4m3fn_x4"), "sa": ("sbuf", [128, 512], "uint8"),
    "uq": ("sbuf", [128, 128], "float8_e4m3fn_x4"), "us": ("sbuf", [128, 128], "uint8"),
    "vq": ("sbuf", [128, 128], "float8_e4m3fn_x4"), "vs": ("sbuf", [128, 128], "uint8"),
    "cq": ("sbuf", [128, 384], "float8_e4m3fn_x4"), "cs": ("sbuf", [128, 384], "uint8"),
    "rq": ("sbuf", [128, 256], "float8_e4m3fn_x4"), "rs": ("sbuf", [128, 256], "uint8"),
    "mq": ("sbuf", [128, 192], "float8_e4m3fn_x4"), "ms": ("sbuf", [128, 384], "uint8"),
    "win": ("sbuf", [128, 2 * RG], "bfloat16"),
    "tile": ("sbuf", [128, 4 * (SL + CAPP)], "bfloat16"),
    "ones": ("sbuf", [128, M3], "bfloat16"), "m6": ("sbuf", [128, ST], "bfloat16"), "m3": ("sbuf", [128, M3], "bfloat16"),
    "ll": ("sbuf", [128, 2, NS], "int32"), "xf": ("sbuf", [128, 4, NS], "float32"), "qq": ("sbuf", [128, 4 * NS], "float32"),
    "sb": ("sbuf", [128, 2 * NS], "int32"), "ee": ("sbuf", [128, 2 * NS], "float32"),
    "dd": ("sbuf", [128, 2 * NS], "float32"), "fd": ("sbuf", [128, 2 * NS], "float32"), "sg": ("sbuf", [128, 2 * NS], "float32"),
    "dq": ("sbuf", [128, 12 * NS + 3], "float32"),
    "of": ("sbuf", [128, 4, 3 * NS], "float32"), "od": ("sbuf", [128, NS], "uint16"), "oo": ("sbuf", [128, 3, 2 * NS], "uint16"),
    "g0": ("sbuf", [128, 8 * SL], "bfloat16"), "g1": ("sbuf", [128, 8 * SL], "bfloat16"), "m4": ("sbuf", [128, 512], "bfloat16"),
    "pl": ("sbuf", [128, 32], "int32"), "pu": ("sbuf", [128, 32], "uint16"),
    "zu": ("sbuf", [128, SL + 1], "float32"), "zv": ("sbuf", [128, SL + 1], "float32"), "zw": ("sbuf", [128, SL + 1], "float32"),
    "gu": ("sbuf", [128, P], "float32"), "yb": ("sbuf", [128, P], "float32"),
    "zp": ("psum", [128, 2048], "float32"), "pp": ("psum", [128, 2048], "float32"),
}
SCRATCH.update({"t%d" % i: ("sbuf", [128, 8 * SL], "bfloat16") for i in range(2)})
SEMAPHORES = ["cv", "cs_", "ct", "cg", "lists", "pfg", "y0", "y1", "arr0", "arr1", "arr2", "sent"] + [w.replace(":", "") for w in LOADS.split() if w[0] != "l"]


def rank_program(g, core, T, topo):
    rank = T.rank_of(core)
    if rank is None:
        return
    A, F = AluOpType, ActivationFunctionType
    que = {"cv": g.vector, "cs_": g.scalar, "ct": g.tensor, "cg": g, "sy": g.sync}
    order = {q: names.split() for q, names in ORDER.items()}
    v, s, t = g.vector, g.scalar, g.tensor
    ts, tt, scan = v.tensor_scalar, v.tensor_tensor, v.tensor_tensor_scan
    pair, mate, odd = rank // 2, rank ^ 1, rank % 2
    eng = topo.engines(core, T.cores[mate])

    pairs = [(pair + k) % 3 for k in ((1, 2, 0) if odd else (0, 2, 1))]

    def cols(c0, c1):
        return (4 * c0, 4 * c1) if odd else (NS - 4 * c1, NS - 4 * c0)

    when = {name: [(q, k + 1)] for q in order for k, name in enumerate(order[q])}
    when.update({"in": [("lists", 32)], "pfg": [("pfg", 256)]})
    when.update({"in" + x[0] + c: [(x.replace(":", ""), 16)] for x in LOADS.split() for c in x[2:]})
    when.update({"arr" + h: [("arr%d" % k, n * len(eng))] for k, (h, n) in enumerate((("a", 2), ("b", 2), ("m", 1)))})
    seen = {q: {} for q in que}
    calls = {}

    def need(q, names):
        for name in names.split():
            for sem, val in when[name]:
                if seen[q].get(sem, 0) < val:
                    que[q].wait_ge(T.sem[sem], val)
                    seen[q][sem] = val

    def call(name, reads, fn, *args, **kw):
        calls[name] = (reads, fn, args, kw)

    def alias(name, *parts):
        if name not in when and all(x in when for x in parts):
            when[name] = [x for part in parts for x in when[part]]

    def copy(name, reads, out, src):
        if name in order["cv"]:
            call(name, reads, v.tensor_copy, out, src)
        else:
            call(name, reads, s.activation, out, src, F.Copy)

    def zero(name, out, n):
        if name in order["cv"]:
            call(name, "", v.memset, out, 0.0)
        elif name in order["cg"]:
            call(name, "one", g.affine_select, out, T.ones[:, 0:n], [[0, n]], A.is_gt, 0.0, 0, 0)
        else:
            call(name, "one", s.activation, out, T.ones[:, 0:n], F.Copy, scale=0.0)

    def line(name, reads, out, src, c, b):
        if name in order["cv"]:
            call(name, reads, ts, out, src, c, b, A.mult, A.add)
        else:
            call(name, reads, s.activation, out, src, F.Identity, bias=b, scale=c)

    for w in LOADS.split():
        q, (x, c) = s if w in ON_SCALAR else g.sync, w.split(":")
        if x == "l":
            q.dma_start(T.ll[:, "no".index(c), :], T[x + c][:]).then_inc(T.sem.lists, 16)
            continue
        a, b = (4 * CUT[c][0], 4 * CUT[c][1]) if x == "x" else (512 * int(c[0]), 512 * int(c[-1]) + 512)
        q.dma_start(T[x + "b"][:, a:b], T[x][:, a:b]).then_inc(T.sem[x + c], 16)
    for k in range(8):
        g.sync.dma_start(T.pl[16 * k:16 * k + 16, 0:16], T.pf[:]).then_inc(T.sem.pfg, 16)
        g.sync.dma_start(T.pl[16 * k:16 * k + 16, 16:32], T.pg[:]).then_inc(T.sem.pfg, 16)

    def at(i):
        return (i // 2) * RG + (i % 2) * ST

    H = 3 * NS
    call("one", "", v.memset, T.ones[:], 1.0)
    D1, D0R = H + 1, 3 * H + 3
    call("c0", "", v.memset, T.dq[:, 0:D1 + H:3], FAR)
    call("c1", "", v.memset, T.dq[:, D1 + H + 2::3], -FAR)
    for i in range(4):
        zero("pad%d" % i, T.win[:, at(i) + H0 + T_COLS:at(i) + H0 + ST], ST - T_COLS)
    zero("zu", T.zu[:, 0:1], 1)
    zero("zv", T.zv[:, 0:1], 1)
    t0 = 0 if odd else CAPP
    zero("tp", T.tile[:, 4 * SL * odd:4 * (SL * odd + CAPP)], 4 * CAPP)
    for b, n in ((B, ST), (3, M3), (4, 512)):
        call("m%d" % b, "one", g.affine_select, T["m%d" % b][:], T.ones[:, 0:n], [[0, n // b], [1, b]], A.is_gt, 0.0, 0, 0)
    lead, tail = E0 + shift(LV), E0 + shift(LV) + B * (NB + USED - 2 ** LV) + 1
    for p in range(2):
        for k, (a, b) in enumerate(((P0 + J, lead), (tail, RG))):
            zero("ez%d" % (2 * p + k), T.win[:, p * RG + a:p * RG + b], b - a)

    lo_, hi_ = slice(0, NS), slice(NS, 2 * NS)
    nb_, q_, q2_, w_ = (T.qq[:, k * NS:(k + 1) * NS] for k in range(4))
    b6_, yy_, x_ = T.dq[:, D1:D1 + 2 * H:3], T.dq[:, D1 + 1:D1 + 2 * H:3], T.xf[:, 1:3, :]
    G0 = E0 - H0
    for k, q in enumerate(pairs):
        o, a = 8 * k, 8 * q
        line("nl%d" % k, "in", T.xf[:, 0:2, o:o + 8], T.ll[:, :, a:a + 8], -1.0, -0.5)
        call("ee%d" % k, "in", tt, T.xf[:, 2, o:o + 8], T.ll[:, 0, a:a + 8], T.ll[:, 1, a:a + 8], A.add)
    alias("nl", "nl0", "nl1", "nl2")
    alias("ee", "ee0", "ee1", "ee2")
    call("sb", "nl ee", ts, T.sb[:], x_, -3.25, 1 / B, A.add, A.mult)
    call("nb", "sb", tt, nb_, T.sb[:, hi_], T.sb[:, lo_], A.add)
    line("b6", "sb", b6_, T.sb[:], 1.0 * B, 0.0)
    call("dd", "b6", tt, T.dd[:], b6_, T.xf[:, 2:0:-1, :], A.add)
    call("sg", "dd", s.activation, T.sg[:], T.dd[:], F.Sign, bias=0.75)
    if "sg" in when:
        line("fd", "sg", T.fd[:], T.sg[:], -J / 2, -J / 2)
    else:
        call("fd", "dd", ts, T.fd[:], T.dd[:], -0.75, -J, A.is_ge, A.mult)
    call("ab0", "fd", tt, T.of[:, 0, 2::3], T.xf[:, 1, :], T.fd[:, lo_], A.subtract)
    line("ej", "ee", T.xf[:, 3, :], T.xf[:, 2, :], 1.0, -1.0 * J)
    call("ab1", "fd ej", tt, T.of[:, 1, 2::3], T.fd[:, hi_], T.xf[:, 3, :], A.subtract)
    line("e0", "nl", T.ee[:, lo_], T.xf[:, 0, :], 1 / 3, G0 + 1.25)
    line("e1", "nl", T.ee[:, hi_], T.xf[:, 0, :], 1 / 3, -G0 - 0.75)
    call("yy", "ee e0 e1", tt, yy_, T.ee[:], x_, A.add)
    call("q", "nb", s.activation, q_, nb_, F.Relu, bias=LIFT, scale=PHI)
    call("q2", "nb", s.activation, q2_, nb_, F.Relu, bias=LIFT - 2.0 ** -11, scale=PHI - 0.5)
    call("w", "q q2", tt, w_, q_, q2_, A.subtract)
    call("tc", "nb", s.activation, T.dq[:, 1:H:3], nb_, F.Relu, bias=2.0 * K, scale=-1.0 * K)
    line("td", "tc", T.dq[:, D0R + 1::3], T.dq[:, 1:H:3], -1.0, 0.0)
    line("ac", "w", T.dq[:, 2:H:3], w_, -1 / 3, J - G0 - 1.0)
    line("ad", "w", T.dq[:, D0R + 2::3], w_, 1 / 3 - B, G0 + 0.25)
    call("of0", "c0 b6 yy tc ac", scan, T.of[:, 2, :], T.dq[:, 0:H], T.dq[:, D1:D1 + H], 0.0, A.add, A.min)
    call("of1", "c1 b6 yy td ad", scan, T.of[:, 3, :], T.dq[:, D0R:], T.dq[:, D1 + H:D1 + 2 * H], 0.0, A.add, A.max)
    left = 1 - odd
    wide = [4 * (b - a) for a, b in SPANS]
    begin = {left: 0, 1 - left: 2 * wide[left], 2: 2 * (wide[0] + wide[1])}

    def offsets(name, o, a, b, j):
        call(name, "ab0 ab1 of0", ts, T.oo[:, :, o:o + b - a], T.of[:, 0:3, 3 * a + 2:3 * b:3], -1, J - 0.75 + ST * j, A.mult, A.add)

    offsets("f00", wide[left], *cols(0, SPANS[1][1]), 0)
    alias("f10", "f00")
    offsets("f20", begin[2], *cols(*SPANS[2]), 0)
    for u, span in enumerate(SPANS):
        offsets("f%d1" % u, begin[u] + wide[u] * (u != left), *cols(*span), 1)
    copy("fx", "of1", T.od[:], T.of[:, 3, 2::3])

    def bank(k, a, b):
        return T.zp[:, 512 * k + a:512 * k + b] if k < 4 else T.pp[:, 512 * (k - 4) + a:512 * (k - 4) + b]

    def cover(name):
        own = [c for c in CUT if name + c in when]
        for c, (a, b) in CUT.items():
            alias(name + c, *[name + d for d in own if CUT[d][0] < b and a < CUT[d][1]])

    cover("qx")
    for c in "ab":
        a, b = CUT[c]
        call("qx" + c, "inx" + c, v.quantize_mx, T.xq[:, a:b], T.xs[:, a:b], T.xb[:, 4 * a:4 * b])
    products = [name for name in order["ct"] if name[0] == "z"]
    for i in range(4):
        w, aq, sa = at(i) + H0, T.aq[:, 128 * i:128 * i + 128], T.sa[:, 128 * i:128 * i + 128]
        call("qa%d" % i, "ina%d" % i, v.quantize_mx, aq, sa, T.ab[:, 512 * i:512 * i + 512])
        for x in "hPS":
            cover(x + str(i))
        for c, (a, b) in CUT.items():
            z = "z%d%s" % (i, c)
            if z in products:
                ps = bank(products.index(z), 0, b - a)
                call(z, "qa%d qx%s" % (i, c), t.matmul_mx, ps, aq, sa, T.xq[:, a:b], T.xs[:, a:b], True, True)
                if "h" + z[1:] in order["cv"]:
                    call("h" + z[1:], z, ts, T.win[:, w + a:w + b], ps, 0.0, 0.05, A.max, A.mult)
                else:
                    call("h" + z[1:], z, s.activation, T.win[:, w + a:w + b], ps, F.Relu, scale=0.05)
            b, reads = b if b < T_COLS else ST, "m6 pad%d h%d%s" % (i, i, c)
            call("P%d%s" % (i, c), reads, scan, T.win[:, w + J + a:w + J + b], T.m6[:, a:b], T.win[:, w + a:w + b], 0.0, A.mult, A.max)
            end = w - J + a - 1 if w - J + a else None
            call("S%d%s" % (i, c), reads, scan, T.win[:, w - J + b - 1:end:-1], T.m6[:, 0:b - a], T.win[:, w + b - 1:w + a - 1:-1], 0.0, A.mult, A.max)
    for p in range(2):
        alias("L%d0" % p, "P%d" % (2 * p), "P%d" % (2 * p + 1), "ez%d" % (2 * p), "ez%d" % (2 * p + 1))
        for m in range(1, LV + 1):
            n = B * (NB + USED - 2 ** m) + 1
            a = p * RG + (E0 + shift(m - 1) if m > 1 else P0 + B - 1)
            b, o = a + B * 2 ** (m - 1), p * RG + E0 + shift(m)
            call("L%d%d" % (p, m), "L%d%d" % (p, m - 1), scan, T.win[:, o:o + n:B], T.win[:, a:a + n:B], T.win[:, b:b + n:B], BIG, A.min, A.max)

    WIN = {"A": (S0, P0), "B": (H0, P0 + J), "C": (H0, RG)}
    named = {x: (x[0], [int(i) for i in x[1:-3]], int(x[-2]), int(x[-1])) for q in ("cv", "cs_") for x in order[q] if ":" in x}

    def over(kinds, i, c0, c1, queue=None):
        return " ".join(x for x, (kind, its, a, b) in named.items()
                        if kind in kinds and set(its) & set(i) and a < c1 and c0 < b and (queue is None or x in order[queue]))

    for name, (x, its, c0, c1) in named.items():
        i, (k0, k1) = its[0], cols(c0, c1)
        p, j = i // 2, i % 2
        w = 4 if over("E", its, c0, c1) else 3
        ta, tb, last = 4 * (t0 + 16 * k0), 4 * (t0 + 16 * k1), T.win[:, at(i) + H0:p * RG + RG].indirect(T.od[:, k0:k1])
        u = [u for u, (a, b) in enumerate(SPANS) if a <= c0 and c1 <= b][0]
        u0, u1 = cols(*SPANS[u])
        a = k0 - u0 + wide[u] * (len(its) == 1 and j != (u == left))
        b = a + len(its) * (k1 - k0)
        gat, top, ga, gb = T["g%d" % p], T["t%d" % p], 128 * u0 + 16 * w * a, 128 * u0 + 16 * w * b
        pa, pb = ga, gb
        if x == "D" and w == 4:
            copy(name, over("s", [0, i], c0, c1), T.tile[:, ta + i:tb:4], top[:, pa + 3:pb:4])
            continue
        if x == "D":
            reads = "fx L%d%d %s %s" % (p, LV, over("s", its, c0, c1), over("C", its, c0, c1, "cv"))
            call(name, reads, tt, T.tile[:, ta + i:tb:4], last, top[:, pa + 2:pb:3], A.max)
            continue
        if x == "s":
            reads, mask = "m%d %s" % (w, over("ABCE", its, c0, c1)), T["m%d" % w][:, 0:gb - ga]
            if w == 4 and i == 0:
                call(name, reads, scan, T.tile[:, tb - 1:ta - 1:-1], mask, gat[:, gb - 1:ga - 1 if ga else None:-1], 0.0, A.mult, A.max)
            else:
                call(name, reads, scan, top[:, pa:pb], mask, gat[:, ga:gb], 0.0, A.mult, A.max)
            continue
        if x == "E":
            call(name, "fx L%d%d" % (p, LV), s.activation, gat[:, ga + 3:gb:4], last, F.Copy)
            continue
        e = "ABC".index(x)
        o = begin[u] + (k0 - u0 + wide[u] * (u == left) if len(its) == 1 else 0)
        src = T.win[:, at(i) + WIN[x][0]:p * RG + WIN[x][1]].indirect(T.oo[:, e, o:o + b - a])
        reads = " ".join("f%d%d" % (u, y) for y in range(len(its))) + " "
        reads += {"A": "S%d S%d" % (2 * p, 2 * p + 1), "B": "P%d P%d" % (2 * p, 2 * p + 1), "C": "L%d%d" % (p, LV)}[x]
        if name in order["cs_"]:
            call(name, reads, s.activation, gat[:, ga + e:gb:w], src, F.Copy)
        else:
            held = gat[:, ga:gb:3] if e == 1 else top[:, pa + 1:pb:3]
            call(name, reads + " " + over("ABC"[e - 1], its, c0, c1), tt, top[:, pa + e:pb:3], src, held, A.max)

    place = {"a": 128 * odd, "b": 128 + 128 * odd, "m": 256 - 256 * odd}
    for h, (c0, c1) in {"a": (0, 2), "b": (2, 4), "m": (3, 5)}.items():
        o, c = place[h], t0 + 16 * cols(c0, c1)[0]
        call("qc" + h, over("D", range(4), c0, c1), v.quantize_mx, T.cq[:, o:o + 128], T.cs[:, o:o + 128], T.tile[:, 4 * c:4 * c + 512])
    c, oq, os_ = (SL - CAPP, CAPP, 256) if odd else (0, 0, 0)
    call("qco", "tp " + over("Ds", range(4), 5, 6), v.quantize_mx, T.mq[:, oq:oq + 128], T.ms[:, os_:os_ + 128], T.tile[:, 4 * c:4 * c + 512])

    call("qu", "inu0", v.quantize_mx, T.uq[:], T.us[:], T.ub[:])
    call("qv", "inv0", v.quantize_mx, T.vq[:], T.vs[:], T.vb[:])
    call("pu", "pfg", ts, T.pu[:], T.pl[:], 1, None, A.add)
    oq, os_ = (0, 192) if odd else (CAPP, CAPP)
    second = {"a": (T.rq[:, 0:128], T.rs[:, 0:128], "arra"), "b": (T.rq[:, 128:256], T.rs[:, 128:256], "arrb"),
              "p": (T.mq[:, oq:oq + 128], T.ms[:, os_:os_ + 128], "qco arrm")}
    for k, (h, (x, xs, reads)) in enumerate(second.items()):
        for j, (name, w, ws, out) in enumerate((("u", T.uq, T.us, T.zu), ("v", T.vq, T.vs, T.zv))):
            call(name.upper() + h, "h0 h1 h2 h3 q%s %s" % (name, reads), t.matmul_mx, bank(2 * k + j, 0, 128), w[:], ws[:], x, xs, True, True)
            o = 128 * ((pair + 2 - k) % 3) + 1
            copy(name + h, name.upper() + h, out[:, o:o + 128], bank(2 * k + j, 0, 128))
        if h != "p":
            copy("w" + h, "u" + h, T.zw[:, o:o + 128], bank(2 * k, 0, 128))
    call("Wp", "h0 h1 h2 h3 qu " + reads, t.matmul_mx, bank(6, 0, 128), T.uq[:], T.us[:], x, xs, True, True)
    copy("wp", "Wp", T.zw[:, o:o + 128], bank(6, 0, 128))
    zero("zw", T.zw[:, 0:1], 1)
    for h in range(2):
        a, b = 128 * h, 128 * h + 128
        x = "w" if "g%d" % h in order["cv"] and "wp" in when else "u"
        copy("g%d" % h, "pu z%s %sa %sb %sp" % ((x,) * 4), T.gu[:, a:b], T["z" + x][:].indirect(T.pu[:, 16 + 8 * h:24 + 8 * h]))
        call("y%d" % h, "pu zv va vb vp g%d" % h, tt, T.yb[:, a:b], T.zv[:].indirect(T.pu[:, 8 * h:8 * h + 8]), T.gu[:, a:b], A.add)

    for q in order:
        for name in order[q]:
            reads, fn, args, kw = calls[name]
            need(q, reads)
            fn(*args, **kw).then_inc(T.sem[q], 1)

    def transfer(r, es, src, out, k):
        rid, pnc = topo.addr(T.cores[r])[0:2]
        return RemoteDMATransfer(dst_ids=[DstId(rid=rid, pnc=pnc)], dma_engine_mask=sum(1 << e for e in es), remote_sem=T.sem["arr%d" % k], src=src, dst=out)

    half = [eng[0::2], eng[1::2]]
    for k, h in enumerate("ab"):
        need("cg", "qc" + h)
        b = 128 * k + CAPP * odd
        ds = [(2 * ((pair + 1 + k) % 3) + j, place[h] + CAPP * j) for j in range(2)]
        g.remote_dma_fused([transfer(r, half[j], T.cq[:, c:c + CAPP].bitcast(dt.uint8), T.rq[:, b:b + CAPP].bitcast(dt.uint8), k)
                            for j, (r, c) in enumerate(ds)], local_sem=T.sem.sent)
        g.remote_dma_fused([transfer(r, half[j], T.cs[:, c:c + CAPP], T.rs[:, b:b + CAPP], k) for j, (r, c) in enumerate(ds)], local_sem=T.sem.sent)
    need("cg", "qca qcb qcm")
    c, b, o = place["m"] + CAPP * odd, 128 * odd, 128 * odd
    g.remote_dma_fused([transfer(mate, half[0], T.cq[:, c:c + CAPP].bitcast(dt.uint8), T.mq[:, b:b + CAPP].bitcast(dt.uint8), 2),
                        transfer(mate, half[1], T.cs[:, CAPP:CAPP + 256], T.ms[:, o:o + 256], 2)], local_sem=T.sem.sent)
    g.wait_ge(T.sem.sent, 5 * len(eng))

    for h, q in enumerate(("sy", "cs_")):
        need(q, "y%d" % h)
        que[q].dma_start(T.y[:, 128 * h:128 * h + 128], T.yb[:, 128 * h:128 * h + 128]).then_inc(T.sem["y%d" % h], 16)
    need("sy", " ".join(order[q][-1] for q in order))
    g.sync.wait_ge(T.sem.y0, 16)
    g.sync.wait_ge(T.sem.y1, 16)
